import numpy as np
import ml_dtypes


def mxq(x, axis, fmt="e4m3"):
    dtype, down = {"e4m3": (ml_dtypes.float8_e4m3fn, 7), "e5m2": (ml_dtypes.float8_e5m2, 14)}[fmt]
    v = np.moveaxis(np.asarray(x, np.float32).astype(ml_dtypes.bfloat16).astype(np.float64), axis, -1)
    blocks = v.reshape(v.shape[:-1] + (-1, 32))
    amax = np.abs(blocks).max(-1, keepdims=True)
    byte = np.maximum(np.where(amax > 0, np.frexp(amax)[1] - 1 + 127, 0) - down, 1)
    scale = np.exp2(byte - 127.0)
    codes = (blocks / scale).astype(np.float32).astype(dtype).astype(np.float64)
    return np.moveaxis((codes * scale).reshape(v.shape), -1, axis)


WIDE = False


def mx_kscale(k):
    if not WIDE:
        return np.ones(k)
    levels = np.array([10, -10, 5, -5, 0])
    if k % 512:
        return np.exp2(np.random.permutation(np.resize(levels, k // 32))).repeat(32)
    a = np.empty((k // 512, 16))
    for p in range(k // 512):
        a[p, :8] = np.random.permutation(np.resize(levels, 8))
        for g in range(8):
            far = levels[np.abs(levels - a[p, g]) >= 10]
            a[p, g + 8] = far[np.random.randint(len(far))]
    return np.exp2(a.ravel()).repeat(32)


def f64(x):
    return np.asarray(x).astype(np.float64)


def striped(idx):
    return np.tile(idx.reshape(-1, 16).T, (8, 1)).astype(np.uint16)


def unstriped(offs):
    return offs[:16].T.reshape(-1).astype(np.int64)


def striped8(idx):
    return np.concatenate([x.reshape(-1, 16).T for x in idx]).astype(np.uint16)


def runs(offs, k):
    lists = np.stack([offs[16 * r : 16 * r + 16].T.reshape(-1) for r in range(8)]).astype(np.int64)
    return lists[np.arange(k) % 512 // 64]


def pack_weight(w):
    k, n = w.shape
    w = f64(np.asarray(w, np.float32).astype(ml_dtypes.bfloat16)).reshape(k // 32, 32, n)
    amax = np.abs(w).max(1)
    byte = np.clip(np.where(amax > 0, np.frexp(amax)[1] - 1 + 127 - 7, 1), 1, 254)
    scaled = (w * np.exp2(127.0 - byte)[:, None, :]).reshape(k, n).astype(np.float32)
    words = np.ascontiguousarray(scaled.reshape(k // 512, 128, 4, n).transpose(0, 1, 3, 2)).astype(ml_dtypes.float8_e4m3fn).view(np.uint8)
    return words, np.ascontiguousarray(byte.astype(np.uint8).reshape(k // 512, 16, n))


def unpack_weight(words, scales):
    g, p, n, _ = words.shape
    vals = np.ascontiguousarray(words).view(ml_dtypes.float8_e4m3fn).astype(np.float64) * np.repeat(np.exp2(scales.astype(np.float64) - 127.0), 8, axis=1)[..., None]
    return vals.transpose(0, 1, 3, 2).reshape(g * 512, n)


E2M1 = np.array([0.0, 0.5, 1.0, 1.5, 2.0, 3.0, 4.0, 6.0, -0.0, -0.5, -1.0, -1.5, -2.0, -3.0, -4.0, -6.0])


def pack_fp4(w):
    k, n = w.shape
    w = f64(np.asarray(w, np.float32).astype(ml_dtypes.bfloat16)).reshape(k // 32, 32, n)
    amax = np.abs(w).max(1)
    mant, ex = np.frexp(amax / 6.0)
    byte = np.clip(np.where(amax > 0, np.where(mant > 0.5, ex, ex - 1) + 127, 1), 1, 254)
    scaled = (w * np.exp2(127.0 - byte)[:, None, :]).reshape(k, n).astype(np.float32)
    c = np.ascontiguousarray(scaled.reshape(k // 512, 128, 4, n).transpose(0, 1, 3, 2)).astype(ml_dtypes.float4_e2m1fn).view(np.uint8) & 0xF
    words = (c[..., 0::2] | (c[..., 1::2] << 4)).reshape(k // 512, 128, 2 * n)
    return np.ascontiguousarray(words), np.ascontiguousarray(byte.astype(np.uint8).reshape(k // 512, 16, n))


def unpack_fp4(words, scales):
    g, _, n = scales.shape
    words = np.ascontiguousarray(words).reshape(g, 128, n, 2)
    nib = np.empty((g, 128, n, 4), np.uint8)
    nib[..., 0::2] = words & 0xF
    nib[..., 1::2] = words >> 4
    vals = E2M1[nib] * np.repeat(np.exp2(scales.astype(np.float64) - 127.0), 8, axis=1)[..., None]
    return vals.transpose(0, 1, 3, 2).reshape(g * 512, n)


def sigmoid(v):
    return 1.0 / (1.0 + np.exp(-np.maximum(v, -700.0)))

def planes(y):
    n, m = y.shape
    v = y.astype(np.float32).astype(ml_dtypes.bfloat16).astype(np.float64).reshape(n // 32, 32, m)
    top = np.abs(v).max(1)
    byte = np.clip(np.where(top > 0, np.frexp(top)[1] - 1 + 127 - 7, 1), 1, 254)
    codes = (v * np.exp2(127.0 - byte)[:, None, :]).reshape(n, m).astype(np.float32).astype(ml_dtypes.float8_e4m3fn).view(np.uint8)
    words = codes.reshape(n // 512, 128, 4, m).transpose(0, 1, 3, 2)
    return np.ascontiguousarray(words), np.ascontiguousarray(byte.astype(np.uint8).reshape(n // 512, 16, m))


K, T, S, H, C = 512, 2048, 512, 512, 512


def setup_inputs():
    n = np.random.standard_normal
    s = mx_kscale(K)[:, None]
    packed_xT = pack_weight(n((K, T)) * s)
    packed_w1 = pack_fp4(n((K, H)) / np.sqrt(K) / s)
    packed_w2 = pack_fp4(n((K, H)) / np.sqrt(K) / s)
    return {
        "x_words": packed_xT[0],
        "x_scales": packed_xT[1],
        "w1_words": packed_w1[0],
        "w1_scales": packed_w1[1],
        "w2_words": packed_w2[0],
        "w2_scales": packed_w2[1],
        "sl": np.random.uniform(1.0, 2.0, (H, 1)).astype(np.float32),
        "th": (0.5 * n((H, 1))).astype(np.float32),
        "gs": (np.random.uniform(0.5, 1.5, (K, 1)) / s).astype(np.float32),
        "tau": np.random.uniform(0.3, 0.9, (C, 1)).astype(np.float32),
        "offs": striped(np.random.permutation(T)[:S]),
        "two": striped(np.random.permutation(T)[:S]),
        "n1": striped8(np.stack([np.random.permutation(S) for _ in range(8)])),
        "n2": striped8(np.stack([np.random.permutation(S) for _ in range(8)])),
        "cand": striped(np.random.permutation(T)[:C]),
        "n3": striped(np.random.permutation(S)),
        "n4": striped(np.random.permutation(S)),
    }


def reference(x_words, x_scales, w1_words, w1_scales, w2_words, w2_scales, sl, th, gs, tau, offs, two, n1, n2, cand, n3, n4):
    x_cand = unpack_weight(x_words, x_scales)[:, unstriped(cand)]
    xq = unpack_weight(x_words, x_scales)[:, unstriped(offs)]
    y = unpack_fp4(w1_words, w1_scales).T @ xq
    x_two = unpack_weight(x_words, x_scales)[:, unstriped(two)]
    d = unpack_fp4(w2_words, w2_scales).T @ x_two
    sg = sigmoid(f64(sl) * (d[np.arange(H)[:, None], runs(n1, H)] - f64(th)))
    z = f64(gs) * (np.maximum(y * sg, d[np.arange(H)[:, None], runs(n2, H)] - d))
    s = 0.0625 * ((x_cand.T @ mxq(z, 0, "e4m3")))
    top = s.max(axis=1, keepdims=True)
    ea = np.exp(f64(tau) * (s[:, unstriped(n3)] - top))
    ea2 = np.exp(f64(tau) * (s[:, unstriped(n4)] - top))
    out_0 = (ea * s[:, unstriped(n3)] + ea2 * s[:, unstriped(n4)]) / (ea + ea2 + 0.125)
    return (out_0,) + planes(out_0)

@@ -1,0 +1,303 @@
+from contextlib import ExitStack
+
+import concourse.mybir as mybir
+
+K, T, S = 512, 2048, 512
+FLOPS = 3 * 2 * 512 * 512 * 512
+
+F32 = mybir.dt.float32
+BF16 = mybir.dt.bfloat16
+I32 = mybir.dt.int32
+U32 = mybir.dt.uint32
+U16 = mybir.dt.uint16
+U8 = mybir.dt.uint8
+FP8X4 = mybir.dt.float8_e4m3fn_x4
+FP4X4 = mybir.dt.float4_e2m1fn_x4
+ALU = mybir.AluOpType
+ACT = mybir.ActivationFunctionType
+
+P = 128
+R = 4
+HALVES = 2
+HW = S // HALVES
+HL = HW // 16
+
+
+def tile_picked_twcmxbevo_none_po_kernel(
+    tc, x_words, x_scales, w1_words, w1_scales, w2_words, w2_scales, sl, th, gs, tau,
+    offs, two, n1, n2, cand, n3, n4, out_0, out_1, out_2,
+):
+    nc = tc.nc
+    with ExitStack() as ctx:
+        sb = ctx.enter_context(tc.tile_pool(name="sb", bufs=1))
+        ps = ctx.enter_context(tc.psum_pool(name="ps", bufs=1))
+
+        def tile(name, shape, dtype, tag=None):
+            return sb.tile(shape, dtype, name=name, tag=tag or name, align_bytes=64)
+
+        def load_list(name, src):
+            dst = tile(name, [P, S // 16], U16)
+            nc.sync.dma_start(dst[:], src)
+            return dst
+
+        def load_scale_rows(queue, dst, src):
+            for q in range(4):
+                queue.dma_start(dst[32 * q : 32 * q + 4, :].bitcast(I32), src[0, 4 * q : 4 * q + 4, :].bitcast(I32))
+
+        def load_column(queue, name, src):
+            dst = tile(name, [P, R], F32)
+            queue.dma_start(dst[:], src.rearrange("(p t) o -> p (t o)", t=R))
+            return dst
+
+        x_sc = tile("x_sc", [P, T], U8)
+        w2_sc_raw = tile("w2_sc_raw", [P, S], U8)
+        w1_sc_raw = tile("w1_sc_raw", [P, S], U8)
+        nc.vector.memset(x_sc[:].bitcast(I32), 0)
+        nc.vector.memset(w2_sc_raw[:].bitcast(I32), 0)
+        nc.vector.memset(w1_sc_raw[:].bitcast(I32), 0)
+
+        sl_c = load_column(nc.gpsimd, "sl_c", sl)
+        th_c = load_column(nc.gpsimd, "th_c", th)
+        two_l = load_list("two_l", two)
+        x_w = tile("x_w", [P, T], U32)
+        x_src = x_words[0].rearrange("p n t -> p (n t)").bitcast(I32)
+        nc.sync.dma_start(x_w[:, : T // 2].bitcast(I32), x_src[:, : T // 2])
+        load_scale_rows(nc.sync, x_sc, x_scales)
+        nc.sync.dma_start(x_w[:, T // 2 :].bitcast(I32), x_src[:, T // 2 :])
+        w2_raw = tile("w2_raw", [P, 2 * S], U8)
+        nc.sync.dma_start(w2_raw[:].bitcast(I32), w2_words[0].bitcast(I32))
+        load_scale_rows(nc.sync, w2_sc_raw, w2_scales)
+        w1_raw = tile("w1_raw", [P, 2 * S], U8)
+        nc.sync.dma_start(w1_raw[:].bitcast(I32), w1_words[0].bitcast(I32))
+        offs_l = load_list("offs_l", offs)
+        n1_l = load_list("n1_l", n1)
+        n2_l = load_list("n2_l", n2)
+        load_scale_rows(nc.sync, w1_sc_raw, w1_scales)
+        cand_l = load_list("cand_l", cand)
+        gs_c = load_column(nc.sync, "gs_c", gs)
+        n3_l = load_list("n3_l", n3)
+        n4_l = load_list("n4_l", n4)
+        tau_c = load_column(nc.sync, "tau_c", tau)
+
+        def gather_scales(name, lst, tag=None):
+            dst = tile(name, [P, S], U8, tag)
+            nc.vector.tensor_copy(dst[:], x_sc[:].indirect(lst[:]))
+            return dst
+
+        def gather_words(name, lst, tag=None):
+            dst = tile(name, [P, S], U32, tag)
+            nc.vector.tensor_copy(dst[:], x_w[:].indirect(lst[:]))
+            return dst
+
+        def deal(copy, dst, src):
+            copy(dst.rearrange("p (t m) -> p t m", t=R), src.rearrange("p (m t) -> p t m", t=R))
+
+        def deal_weight(name, raw, sc_raw, scale_engine):
+            w = tile(name, [P, 2 * S], U8)
+            sc = tile(name + "_sc", [P, S], U8)
+            deal(nc.scalar.copy, w[:].bitcast(U16), raw[:].bitcast(U16))
+            deal(scale_engine.tensor_copy, sc[:], sc_raw[:])
+            return w, sc
+
+        def project(tag, w, sc, xw, xs):
+            banks = []
+            for t in range(R):
+                bank = ps.tile([P, S], F32, name=f"{tag}{t}", tag=f"{tag}{t}")
+                nc.tensor.matmul_mx(
+                    out=bank[:],
+                    lhsT=w[:, 2 * P * t : 2 * P * (t + 1)].bitcast(FP4X4),
+                    lhsT_scale=sc[:, P * t : P * (t + 1)],
+                    rhs=xw[:].bitcast(FP8X4),
+                    rhs_scale=xs[:],
+                    start=True,
+                    stop=True,
+                )
+                banks.append(bank)
+            return banks
+
+        two_s = gather_scales("two_s", two_l)
+        two_w = gather_words("two_w", two_l)
+        w2, w2_sc = deal_weight("w2", w2_raw, w2_sc_raw, nc.gpsimd)
+        d_ps = project("a", w2, w2_sc, two_w, two_s)
+
+        sig_bias = tile("sig_bias", [P, R], F32)
+        sl_th = tile("sl_th", [P, R], F32)
+        nc.gpsimd.tensor_tensor(sl_th[:], sl_c[:], th_c[:], ALU.mult)
+        nc.gpsimd.tensor_scalar(sig_bias[:], sl_th[:], -1.0, 0.0, ALU.mult, ALU.add)
+
+        offs_s = gather_scales("offs_s", offs_l)
+        offs_w = gather_words("offs_w", offs_l)
+        w1, w1_sc = deal_weight("w1", w1_raw, w1_sc_raw, nc.gpsimd)
+        y_ps = project("b", w1, w1_sc, offs_w, offs_s)
+
+        cand_s_raw = gather_scales("cand_s_raw", cand_l)
+        cand_w_raw = gather_words("cand_w_raw", cand_l)
+        cand_s = tile("cand_s", [P, S], U8)
+        cand_w = tile("cand_w", [P, S], U32)
+        deal(nc.vector.tensor_copy, cand_s[:], cand_s_raw[:])
+        deal(nc.vector.tensor_copy, cand_w[:], cand_w_raw[:])
+
+        def interleave(dst, src, copy=nc.vector.tensor_copy):
+            copy(
+                dst.rearrange("p (c i) t -> p c t i", i=4), src.rearrange("p t (c i) -> p c t i", i=4)
+            )
+
+        def quantise(words, scales, src):
+            nc.vector.quantize_mx(out=words.bitcast(FP8X4), scales=scales, in_=src.rearrange("p n t -> p (n t)"))
+
+        def run_staggered(chains):
+            for step in range(len(chains) + 2):
+                for stage in (0, 2, 4, 1, 3, 5):
+                    i = step - stage // 2
+                    if 0 <= i < len(chains) and stage < len(chains[i]):
+                        chains[i][stage]()
+
+        full = (slice(0, S), slice(0, S // 16))
+        halves = [(slice(HW * h, HW * (h + 1)), slice(HL * h, HL * (h + 1))) for h in range(HALVES)]
+
+        z_w = tile("z_w", [P, S], U32)
+        z_s = tile("z_s", [P, S], U8)
+        chunks = ((0, 256), (256, 384), (384, 512))
+        z_planes = {c0: tile(f"z_planes{c0}", [P, R, c1 - c0], BF16) for c0, c1 in chunks}
+        d_sb = [tile(f"d_sb{t}", [P, S], F32) for t in range(R)]
+        win = [tile(f"win{t}", [P, 2 * S], F32) for t in range(R)]
+
+        sg_tiles = []
+
+        def z_chain(t, c0, c1):
+            cols, lcols = slice(c0, c1), slice(c0 // 16, c1 // 16)
+            gated = win[t][:, S + c0 : S + c1]
+            last = t == R - 1
+            sg = tile(f"sg{t}_{c0}", [P, c1 - c0], F32)
+            far = tile(f"far{t}_{c0}", [P, c1 - c0], F32)
+            diff = sg_tiles[-1][:, : c1 - c0] if sg_tiles else tile("diff_first", [P, c1 - c0], F32, "cand_w_raw")[:]
+            sg_tiles.append(sg)
+            big = tile(f"big{t}_{c0}", [P, c1 - c0], F32)
+
+            def gate():
+                if c0 == 0:
+                    nc.scalar.copy(d_sb[t][:], d_ps[t][:])
+                nc.scalar.activation(sg[:], d_sb[t][:].indirect(n1_l[:, lcols]), ACT.Sigmoid,
+                                     bias=sig_bias[:, t : t + 1], scale=sl_c[:, t : t + 1])
+                nc.vector.tensor_tensor(gated, y_ps[t][:, cols], sg[:], ALU.mult)
+
+            def differ():
+                nc.scalar.activation(far[:], d_sb[t][:].indirect(n2_l[:, lcols]), ACT.Copy)
+                nc.vector.tensor_tensor(diff, far[:], d_ps[t][:, cols], ALU.subtract)
+
+            def weigh():
+                for a0, a1 in chunks:
+                    if c0 <= a0 < c1:
+                        (nc.vector if last else nc.gpsimd).tensor_scalar(
+                            z_planes[a0][:, t, :], big[:, a0 - c0 : a1 - c0], gs_c[:, t : t + 1], 0.0, ALU.mult, ALU.add)
+
+            steps = [gate, differ, lambda: nc.vector.tensor_tensor(big[:], gated, diff, ALU.max), weigh]
+            if last:
+                z_bf = tile(f"z_bf{c0}", [P, c1 - c0, R], BF16)
+                steps.append(lambda: interleave(z_bf[:], z_planes[c0][:]))
+                steps.append(lambda: quantise(z_w[:, cols], z_s[:, cols], z_bf[:]))
+            return steps
+
+        run_staggered(
+            [z_chain(t, 0, HW) for t in range(R)]
+            + [z_chain(t, HW, S) for t in range(R - 1)]
+            + [z_chain(R - 1, c0, c1) for c0, c1 in chunks[1:]]
+        )
+
+        EARLY = 1
+        ea = [tile(f"ea{t}", [P, S], F32) for t in range(R)]
+        eb = [tile(f"eb{t}", [P, S], F32) for t in range(R)]
+        den_sq = [tile(f"den_sq{h}", [P, R, HW], F32) for h in range(HALVES)]
+        inv = [tile(f"inv{h}", [P, R, HW], F32) for h in range(HALVES)]
+        res = {c0: tile(f"res{c0}", [P, R, c1 - c0], F32) for c0, c1 in chunks}
+        o_w = tile("o_w", [P, S], U32)
+        o_s = tile("o_s", [P, S], U8)
+        out_rows = out_0.rearrange("(p t) n -> p t n", t=R)
+        out_words = out_1[0].rearrange("p n t -> p (n t)").bitcast(I32)
+        out_scales = out_2[0].bitcast(I32)
+
+        def fetch_product(prod, weight, lst, t, c0, c1, fetched):
+            nc.scalar.activation(fetched, win[t][:].indirect(lst[:, c0 // 16 : c1 // 16]), ACT.Copy)
+            nc.vector.tensor_tensor(prod, weight[t][:, c0:c1], fetched, ALU.mult)
+
+        for t in range(R):
+            bank = ps.tile([P, S], F32, name=f"s{t}", tag=f"a{t}")
+            for c0, c1 in chunks:
+                nc.tensor.matmul_mx(
+                    out=bank[:, c0:c1],
+                    lhsT=cand_w[:, P * t : P * (t + 1)].bitcast(FP8X4),
+                    lhsT_scale=cand_s[:, P * t : P * (t + 1)],
+                    rhs=z_w[:, c0:c1].bitcast(FP8X4),
+                    rhs_scale=z_s[:, c0:c1],
+                    start=True,
+                    stop=True,
+                )
+            top = tile(f"top{t}", [P, 1], F32)
+            bias = tile(f"exp_bias{t}", [P, 1], F32)
+            nc.vector.tensor_scalar(win[t][:, :S], bank[:], 0.0625, None, ALU.mult, ALU.max, accum_out=top[:])
+            nc.vector.tensor_scalar(bias[:], top[:], tau_c[:, t : t + 1], -1.0, ALU.mult, ALU.mult)
+            for dst, lst in ((ea, n3_l), (eb, n4_l)):
+                nc.scalar.activation(dst[t][:], win[t][:].indirect(lst[:]), ACT.Exp,
+                                     bias=bias[:], scale=tau_c[:, t : t + 1])
+        early = tile("early", [P, EARLY, 2, S], F32, "exp_bias3")
+        early_pa = tile("early_pa", [P, EARLY, S], F32)
+        early_pb = tile("early_pb", [P, EARLY, S], F32)
+        early_num = tile("early_num", [P, EARLY, S], F32)
+        for t in range(R):
+            den = [tile(f"den{t}_{h}", [P, HW], F32) for h in range(HALVES)]
+            for h in range(HALVES):
+                cols = slice(HW * h, HW * (h + 1))
+                nc.vector.scalar_tensor_tensor(den[h][:], ea[t][:, cols], 0.125, eb[t][:, cols], ALU.add, ALU.add)
+            for h in range(HALVES):
+                nc.vector.tensor_tensor(den_sq[h][:, t, :], den[h][:], den[h][:], ALU.mult)
+            if t < EARLY:
+                fetch_product(early_pa[:, t, :], ea, n3_l, t, 0, S, early[:, t, 0, :])
+                fetch_product(early_pb[:, t, :], eb, n4_l, t, 0, S, early[:, t, 1, :])
+        nc.vector.tensor_tensor(early_num[:], early_pa[:], early_pb[:], ALU.add)
+        for h in range(HALVES):
+            nc.scalar.activation(inv[h][:], den_sq[h][:], ACT.Abs_reciprocal_sqrt)
+
+        def divide(tiles, c0, c1, num):
+            part = slice(c0 % HW, c0 % HW + c1 - c0)
+            nc.vector.tensor_tensor(res[c0][:, tiles, :], num, inv[c0 // HW][:, tiles, part], ALU.mult)
+            nc.sync.dma_start(out_rows[:, tiles, c0:c1], res[c0][:, tiles, :])
+
+        def finish(c0, c1, res_bf):
+            quantise(o_w[:, c0:c1], o_s[:, c0:c1], res_bf[:])
+            nc.sync.dma_start(out_words[:, c0:c1], o_w[:, c0:c1].bitcast(I32))
+
+        fetched = []
+        late = []
+
+        def out_chain(c0, c1, t):
+            spent, part = den_sq[c0 // HW], slice(c0 % HW, c0 % HW + c1 - c0)
+            at_n3 = spent[:, t, part]
+            at_n4 = fetched[-2][:, : c1 - c0] if len(fetched) > 1 else den_sq[len(fetched)][:, 0, :]
+            fetched.append(at_n3)
+            pa = tile(f"pa{t}_{c0}", [P, c1 - c0], F32)
+            pb = tile(f"pb{t}_{c0}", [P, c1 - c0], F32)
+            num = tile(f"num{t}_{c0}", [P, c1 - c0], F32)
+            steps = [
+                lambda: fetch_product(pa[:], ea, n3_l, t, c0, c1, at_n3),
+                lambda: fetch_product(pb[:], eb, n4_l, t, c0, c1, at_n4),
+                lambda: nc.vector.tensor_tensor(num[:], pa[:], pb[:], ALU.add),
+                lambda: divide(slice(t, t + 1), c0, c1, num[:].unsqueeze(1)),
+            ]
+            if t == R - 1:
+                res_bf = tile(f"res_bf{c0}", [P, c1 - c0, R], BF16)
+                if c0 == 0:
+                    late.append(lambda: interleave(res_bf[:], res[c0][:], nc.scalar.copy))
+                    late.append(lambda: finish(c0, c1, res_bf))
+                else:
+                    steps.append(lambda: interleave(res_bf[:], res[c0][:]))
+                    steps.append(lambda: finish(c0, c1, res_bf))
+            return steps
+
+        for c0, c1 in chunks:
+            divide(slice(0, EARLY), c0, c1, early_num[:, :, c0:c1])
+        run_staggered([out_chain(c0, c1, t) for c0, c1 in chunks for t in range(EARLY, R)])
+        for step in late:
+            step()
+        for q in range(4):
+            queue = nc.scalar if q % 2 else nc.sync
+            queue.dma_start(out_scales[4 * q : 4 * q + 4, :], o_s[32 * q : 32 * q + 4, :].bitcast(I32))

@@ -56,6 +56,9 @@ def tile_picked_twcmxbevo_none_po_kernel(
         nc.vector.memset(w2_sc_raw[:].bitcast(I32), 0)
         nc.vector.memset(w1_sc_raw[:].bitcast(I32), 0)
 
+        warm = tile("warm", [P, 2], F32)
+        nc.gpsimd.memset(warm[:, 0:1], 0.0)
+        nc.scalar.activation(warm[:, 1:2], warm[:, 0:1], ACT.Sigmoid)
         sl_c = load_column(nc.gpsimd, "sl_c", sl)
         th_c = load_column(nc.gpsimd, "th_c", th)
         two_l = load_list("two_l", two)

@@ -40,8 +40,8 @@ def tile_picked_twcmxbevo_none_po_kernel(
             nc.sync.dma_start(dst[:], src)
             return dst
 
-        def load_scale_rows(queue, dst, src):
-            for q in range(4):
+        def load_scale_rows(queues, dst, src):
+            for q, queue in enumerate(queues):
                 queue.dma_start(dst[32 * q : 32 * q + 4, :].bitcast(I32), src[0, 4 * q : 4 * q + 4, :].bitcast(I32))
 
         def load_column(queue, name, src):
@@ -65,17 +65,17 @@ def tile_picked_twcmxbevo_none_po_kernel(
         x_w = tile("x_w", [P, T], U32)
         x_src = x_words[0].rearrange("p n t -> p (n t)").bitcast(I32)
         nc.sync.dma_start(x_w[:, : T // 2].bitcast(I32), x_src[:, : T // 2])
-        load_scale_rows(nc.sync, x_sc, x_scales)
+        load_scale_rows([nc.sync] * 4, x_sc, x_scales)
         nc.sync.dma_start(x_w[:, T // 2 :].bitcast(I32), x_src[:, T // 2 :])
         w2_raw = tile("w2_raw", [P, 2 * S], U8)
         nc.sync.dma_start(w2_raw[:].bitcast(I32), w2_words[0].bitcast(I32))
-        load_scale_rows(nc.sync, w2_sc_raw, w2_scales)
+        load_scale_rows([nc.sync] * 4, w2_sc_raw, w2_scales)
         w1_raw = tile("w1_raw", [P, 2 * S], U8)
         nc.sync.dma_start(w1_raw[:].bitcast(I32), w1_words[0].bitcast(I32))
         offs_l = load_list("offs_l", offs)
         n1_l = load_list("n1_l", n1)
         n2_l = load_list("n2_l", n2)
-        load_scale_rows(nc.sync, w1_sc_raw, w1_scales)
+        load_scale_rows([nc.sync] * 4, w1_sc_raw, w1_scales)
         cand_l = load_list("cand_l", cand)
         gs_c = load_column(nc.sync, "gs_c", gs)
         n3_l = load_list("n3_l", n3)
@@ -87,41 +87,45 @@ def tile_picked_twcmxbevo_none_po_kernel(
             nc.vector.tensor_copy(dst[:], x_sc[:].indirect(lst[:]))
             return dst
 
-        def gather_words(name, lst, tag=None):
+        def gather_words(name, lst, parts=1, tag=None):
             dst = tile(name, [P, S], U32, tag)
-            nc.vector.tensor_copy(dst[:], x_w[:].indirect(lst[:]))
+            for h in range(parts):
+                w = S // parts
+                nc.vector.tensor_copy(dst[:, w * h : w * (h + 1)], x_w[:].indirect(lst[:, w * h // 16 : w * (h + 1) // 16]))
             return dst
 
         def deal(copy, dst, src):
             copy(dst.rearrange("p (t m) -> p t m", t=R), src.rearrange("p (m t) -> p t m", t=R))
 
-        def deal_weight(name, raw, sc_raw, scale_engine):
+        def deal_weight(name, raw, sc_raw):
             w = tile(name, [P, 2 * S], U8)
             sc = tile(name + "_sc", [P, S], U8)
             deal(nc.scalar.copy, w[:].bitcast(U16), raw[:].bitcast(U16))
-            deal(scale_engine.tensor_copy, sc[:], sc_raw[:])
+            deal(nc.vector.tensor_copy, sc[:], sc_raw[:])
             return w, sc
 
-        def project(tag, w, sc, xw, xs):
+        def project(tag, w, sc, xw, xs, parts=1):
             banks = []
             for t in range(R):
                 bank = ps.tile([P, S], F32, name=f"{tag}{t}", tag=f"{tag}{t}")
-                nc.tensor.matmul_mx(
-                    out=bank[:],
-                    lhsT=w[:, 2 * P * t : 2 * P * (t + 1)].bitcast(FP4X4),
-                    lhsT_scale=sc[:, P * t : P * (t + 1)],
-                    rhs=xw[:].bitcast(FP8X4),
-                    rhs_scale=xs[:],
-                    start=True,
-                    stop=True,
-                )
+                n = S // (parts if t == 0 else 1)
+                for c0 in range(0, S, n):
+                    nc.tensor.matmul_mx(
+                        out=bank[:, c0 : c0 + n],
+                        lhsT=w[:, 2 * P * t : 2 * P * (t + 1)].bitcast(FP4X4),
+                        lhsT_scale=sc[:, P * t : P * (t + 1)],
+                        rhs=xw[:, c0 : c0 + n].bitcast(FP8X4),
+                        rhs_scale=xs[:, c0 : c0 + n],
+                        start=True,
+                        stop=True,
+                    )
                 banks.append(bank)
             return banks
 
         two_s = gather_scales("two_s", two_l)
-        two_w = gather_words("two_w", two_l)
-        w2, w2_sc = deal_weight("w2", w2_raw, w2_sc_raw, nc.gpsimd)
-        d_ps = project("a", w2, w2_sc, two_w, two_s)
+        two_w = gather_words("two_w", two_l, HALVES)
+        w2, w2_sc = deal_weight("w2", w2_raw, w2_sc_raw)
+        d_ps = project("a", w2, w2_sc, two_w, two_s, HALVES)
 
         sig_bias = tile("sig_bias", [P, R], F32)
         sl_th = tile("sl_th", [P, R], F32)
@@ -130,7 +134,7 @@ def tile_picked_twcmxbevo_none_po_kernel(
 
         offs_s = gather_scales("offs_s", offs_l)
         offs_w = gather_words("offs_w", offs_l)
-        w1, w1_sc = deal_weight("w1", w1_raw, w1_sc_raw, nc.gpsimd)
+        w1, w1_sc = deal_weight("w1", w1_raw, w1_sc_raw)
         y_ps = project("b", w1, w1_sc, offs_w, offs_s)
 
         cand_s_raw = gather_scales("cand_s_raw", cand_l)
@@ -138,7 +142,9 @@ def tile_picked_twcmxbevo_none_po_kernel(
         cand_s = tile("cand_s", [P, S], U8)
         cand_w = tile("cand_w", [P, S], U32)
         deal(nc.vector.tensor_copy, cand_s[:], cand_s_raw[:])
-        deal(nc.vector.tensor_copy, cand_w[:], cand_w_raw[:])
+        nc.vector.tensor_copy(
+            cand_w[:].rearrange("p (t m) -> p m t", t=R), cand_w_raw[:].rearrange("p (m t) -> p m t", t=R)
+        )
 
         def interleave(dst, src, copy=nc.vector.tensor_copy):
             copy(
@@ -207,11 +213,12 @@ def tile_picked_twcmxbevo_none_po_kernel(
             + [z_chain(R - 1, c0, c1) for c0, c1 in chunks[1:]]
         )
 
-        EARLY = 1
+        neg_tau = tile("neg_tau", [P, R], F32)
+        nc.gpsimd.tensor_scalar(neg_tau[:], tau_c[:], -1.0, 0.0, ALU.mult, ALU.add)
         ea = [tile(f"ea{t}", [P, S], F32) for t in range(R)]
         eb = [tile(f"eb{t}", [P, S], F32) for t in range(R)]
-        den_sq = [tile(f"den_sq{h}", [P, R, HW], F32) for h in range(HALVES)]
-        inv = [tile(f"inv{h}", [P, R, HW], F32) for h in range(HALVES)]
+        den_sq = [tile(f"den_sq{h}", [P, R - 1, HW], F32) for h in range(HALVES)]
+        inv = [tile(f"inv{h}", [P, R - 1, HW], F32) for h in range(HALVES)]
         res = {c0: tile(f"res{c0}", [P, R, c1 - c0], F32) for c0, c1 in chunks}
         o_w = tile("o_w", [P, S], U32)
         o_s = tile("o_s", [P, S], U8)
@@ -219,51 +226,72 @@ def tile_picked_twcmxbevo_none_po_kernel(
         out_words = out_1[0].rearrange("p n t -> p (n t)").bitcast(I32)
         out_scales = out_2[0].bitcast(I32)
 
-        def fetch_product(prod, weight, lst, t, c0, c1, fetched):
-            nc.scalar.activation(fetched, win[t][:].indirect(lst[:, c0 // 16 : c1 // 16]), ACT.Copy)
-            nc.vector.tensor_tensor(prod, weight[t][:, c0:c1], fetched, ALU.mult)
+        def score(t, bank, c0, c1):
+            nc.tensor.matmul_mx(
+                out=bank,
+                lhsT=cand_w[:, P * t : P * (t + 1)].bitcast(FP8X4),
+                lhsT_scale=cand_s[:, P * t : P * (t + 1)],
+                rhs=z_w[:, c0:c1].bitcast(FP8X4),
+                rhs_scale=z_s[:, c0:c1],
+                start=True,
+                stop=True,
+            )
+
+        def leave_psum(name, t, bank, c0, c1):
+            top = tile(name, [P, 1], F32)
+            nc.vector.tensor_scalar(win[t][:, c0:c1], bank, 0.0625, None, ALU.mult, ALU.max, accum_out=top[:])
+            return top
 
         for t in range(R):
             bank = ps.tile([P, S], F32, name=f"s{t}", tag=f"a{t}")
-            for c0, c1 in chunks:
-                nc.tensor.matmul_mx(
-                    out=bank[:, c0:c1],
-                    lhsT=cand_w[:, P * t : P * (t + 1)].bitcast(FP8X4),
-                    lhsT_scale=cand_s[:, P * t : P * (t + 1)],
-                    rhs=z_w[:, c0:c1].bitcast(FP8X4),
-                    rhs_scale=z_s[:, c0:c1],
-                    start=True,
-                    stop=True,
-                )
-            top = tile(f"top{t}", [P, 1], F32)
             bias = tile(f"exp_bias{t}", [P, 1], F32)
-            nc.vector.tensor_scalar(win[t][:, :S], bank[:], 0.0625, None, ALU.mult, ALU.max, accum_out=top[:])
-            nc.vector.tensor_scalar(bias[:], top[:], tau_c[:, t : t + 1], -1.0, ALU.mult, ALU.mult)
+            if t == 0:
+                side = ps.tile([P, S], F32, name="s0_side", tag="b0")
+                score(t, side[:, :HW], 0, HW)
+                top_a = leave_psum("top0a", t, side[:, :HW], 0, HW)
+                for c0, c1 in chunks[1:]:
+                    score(t, bank[:, c0:c1], c0, c1)
+                top_b = leave_psum("top0b", t, bank[:, HW:], HW, S)
+                nc.vector.tensor_scalar(bias[:], top_b[:], top_a[:], neg_tau[:, t : t + 1], ALU.max, ALU.mult)
+            else:
+                score(t, bank[:], 0, S)
+                top = leave_psum(f"top{t}", t, bank[:], 0, S)
+                nc.vector.tensor_tensor(bias[:], top[:], neg_tau[:, t : t + 1], ALU.mult)
             for dst, lst in ((ea, n3_l), (eb, n4_l)):
                 nc.scalar.activation(dst[t][:], win[t][:].indirect(lst[:]), ACT.Exp,
                                      bias=bias[:], scale=tau_c[:, t : t + 1])
-        early = tile("early", [P, EARLY, 2, S], F32, "exp_bias3")
-        early_pa = tile("early_pa", [P, EARLY, S], F32)
-        early_pb = tile("early_pb", [P, EARLY, S], F32)
-        early_num = tile("early_num", [P, EARLY, S], F32)
+
+        def fetch_product(prod, weight, lst, t, c0, c1, fetched):
+            nc.scalar.activation(fetched, win[t][:].indirect(lst[:, c0 // 16 : c1 // 16]), ACT.Copy)
+            nc.vector.tensor_tensor(prod, weight, fetched, ALU.mult)
+
+        def store_rows(t, c0, c1):
+            nc.sync.dma_start(out_rows[:, t, c0:c1], res[c0][:, t, :])
+
+        inv0 = tile("inv0", [P, S], F32)
+        den = {}
         for t in range(R):
-            den = [tile(f"den{t}_{h}", [P, HW], F32) for h in range(HALVES)]
             for h in range(HALVES):
                 cols = slice(HW * h, HW * (h + 1))
-                nc.vector.scalar_tensor_tensor(den[h][:], ea[t][:, cols], 0.125, eb[t][:, cols], ALU.add, ALU.add)
+                den[t, h] = tile(f"den{t}_{h}", [P, HW], F32)
+                nc.vector.scalar_tensor_tensor(den[t, h][:], ea[t][:, cols], 0.125, eb[t][:, cols], ALU.add, ALU.add)
             for h in range(HALVES):
-                nc.vector.tensor_tensor(den_sq[h][:, t, :], den[h][:], den[h][:], ALU.mult)
-            if t < EARLY:
-                fetch_product(early_pa[:, t, :], ea, n3_l, t, 0, S, early[:, t, 0, :])
-                fetch_product(early_pb[:, t, :], eb, n4_l, t, 0, S, early[:, t, 1, :])
-        nc.vector.tensor_tensor(early_num[:], early_pa[:], early_pb[:], ALU.add)
+                if t == 0:
+                    nc.vector.reciprocal(inv0[:, HW * h : HW * (h + 1)], den[t, h][:])
+                else:
+                    nc.vector.tensor_tensor(den_sq[h][:, t - 1, :], den[t, h][:], den[t, h][:], ALU.mult)
+        early = tile("early", [P, 2, S], F32, "exp_bias3")
+        pa0 = tile("pa0", [P, S], F32)
+        pb0 = tile("pb0", [P, S], F32)
+        num0 = tile("num0", [P, S], F32)
+        fetch_product(pa0[:], ea[0][:], n3_l, 0, 0, S, early[:, 0, :])
+        fetch_product(pb0[:], eb[0][:], n4_l, 0, 0, S, early[:, 1, :])
+        nc.vector.tensor_tensor(num0[:], pa0[:], pb0[:], ALU.add)
+        for c0, c1 in chunks:
+            nc.vector.tensor_tensor(res[c0][:, 0, :], num0[:, c0:c1], inv0[:, c0:c1], ALU.mult)
+            store_rows(0, c0, c1)
         for h in range(HALVES):
             nc.scalar.activation(inv[h][:], den_sq[h][:], ACT.Abs_reciprocal_sqrt)
-
-        def divide(tiles, c0, c1, num):
-            part = slice(c0 % HW, c0 % HW + c1 - c0)
-            nc.vector.tensor_tensor(res[c0][:, tiles, :], num, inv[c0 // HW][:, tiles, part], ALU.mult)
-            nc.sync.dma_start(out_rows[:, tiles, c0:c1], res[c0][:, tiles, :])
 
         def finish(c0, c1, res_bf):
             quantise(o_w[:, c0:c1], o_s[:, c0:c1], res_bf[:])
@@ -271,34 +299,57 @@ def tile_picked_twcmxbevo_none_po_kernel(
 
         fetched = []
         late = []
+        share_a = tile("share_a", [P, HW], F32)
+        share_b = tile("share_b", [P, HW], F32)
 
-        def out_chain(c0, c1, t):
-            spent, part = den_sq[c0 // HW], slice(c0 % HW, c0 % HW + c1 - c0)
-            at_n3 = spent[:, t, part]
-            at_n4 = fetched[-2][:, : c1 - c0] if len(fetched) > 1 else den_sq[len(fetched)][:, 0, :]
+        def out_chain(t, c0, c1):
+            h, part = c0 // HW, slice(c0 % HW, c0 % HW + c1 - c0)
+            at_n3 = den_sq[h][:, t - 1, part]
+            at_n4 = (fetched[-2] if len(fetched) > 1 else den[R - 1, len(fetched)][:])[:, : c1 - c0]
             fetched.append(at_n3)
             pa = tile(f"pa{t}_{c0}", [P, c1 - c0], F32)
             pb = tile(f"pb{t}_{c0}", [P, c1 - c0], F32)
+            if t == R - 1 and h == 1:
+
+                def add_up():
+                    nc.vector.tensor_tensor(res[c0][:, t, :], pa[:], pb[:], ALU.add)
+                    store_rows(t, c0, c1)
+
+                res_bf = tile(f"res_bf{c0}", [P, c1 - c0, R], BF16)
+                return [
+                    lambda: fetch_product(pa[:], share_a[:, part], n3_l, t, c0, c1, at_n3),
+                    lambda: fetch_product(pb[:], share_b[:, part], n4_l, t, c0, c1, at_n4),
+                    add_up,
+                    lambda: interleave(res_bf[:], res[c0][:]),
+                    lambda: finish(c0, c1, res_bf),
+                ]
             num = tile(f"num{t}_{c0}", [P, c1 - c0], F32)
-            steps = [
-                lambda: fetch_product(pa[:], ea, n3_l, t, c0, c1, at_n3),
-                lambda: fetch_product(pb[:], eb, n4_l, t, c0, c1, at_n4),
-                lambda: nc.vector.tensor_tensor(num[:], pa[:], pb[:], ALU.add),
-                lambda: divide(slice(t, t + 1), c0, c1, num[:].unsqueeze(1)),
-            ]
+
+            def divide():
+                for a0, a1 in chunks:
+                    if c0 <= a0 < c1:
+                        nc.vector.tensor_tensor(
+                            res[a0][:, t, :], num[:, a0 - c0 : a1 - c0], inv[h][:, t - 1, a0 - HW * h : a1 - HW * h], ALU.mult)
+                        store_rows(t, a0, a1)
+
             if t == R - 1:
                 res_bf = tile(f"res_bf{c0}", [P, c1 - c0, R], BF16)
-                if c0 == 0:
-                    late.append(lambda: interleave(res_bf[:], res[c0][:], nc.scalar.copy))
-                    late.append(lambda: finish(c0, c1, res_bf))
-                else:
-                    steps.append(lambda: interleave(res_bf[:], res[c0][:]))
-                    steps.append(lambda: finish(c0, c1, res_bf))
-            return steps
+                late.append(lambda: interleave(res_bf[:], res[c0][:], nc.scalar.copy))
+                late.append(lambda: finish(c0, c1, res_bf))
+            return [
+                lambda: fetch_product(pa[:], ea[t][:, c0:c1], n3_l, t, c0, c1, at_n3),
+                lambda: fetch_product(pb[:], eb[t][:, c0:c1], n4_l, t, c0, c1, at_n4),
+                lambda: nc.vector.tensor_tensor(num[:], pa[:], pb[:], ALU.add),
+                divide,
+            ]
 
-        for c0, c1 in chunks:
-            divide(slice(0, EARLY), c0, c1, early_num[:, :, c0:c1])
-        run_staggered([out_chain(c0, c1, t) for c0, c1 in chunks for t in range(EARLY, R)])
+        nc.vector.tensor_tensor(share_a[:], ea[R - 1][:, HW:], inv[1][:, R - 2, :], ALU.mult)
+        nc.vector.tensor_tensor(share_b[:], eb[R - 1][:, HW:], inv[1][:, R - 2, :], ALU.mult)
+        run_staggered(
+            [out_chain(t, 0, HW) for t in range(1, R)]
+            + [out_chain(t, HW, S) for t in range(1, R - 1)]
+            + [out_chain(R - 1, c0, c1) for c0, c1 in chunks[1:]]
+        )
         for step in late:
             step()
         for q in range(4):

@@ -158,7 +158,7 @@ def tile_picked_twcmxbevo_none_po_kernel(
             for step in range(len(chains) + 2):
                 for stage in (0, 2, 4, 1, 3, 5):
                     i = step - stage // 2
-                    if 0 <= i < len(chains) and stage < len(chains[i]):
+                    if 0 <= i < len(chains) and stage < len(chains[i]) and chains[i][stage]:
                         chains[i][stage]()
 
         full = (slice(0, S), slice(0, S // 16))
@@ -217,9 +217,6 @@ def tile_picked_twcmxbevo_none_po_kernel(
         nc.gpsimd.tensor_scalar(neg_tau[:], tau_c[:], -1.0, 0.0, ALU.mult, ALU.add)
         ea = [tile(f"ea{t}", [P, S], F32) for t in range(R)]
         eb = [tile(f"eb{t}", [P, S], F32) for t in range(R)]
-        den_sq = [tile(f"den_sq{h}", [P, R - 1, HW], F32) for h in range(HALVES)]
-        inv = [tile(f"inv{h}", [P, R - 1, HW], F32) for h in range(HALVES)]
-        res = {c0: tile(f"res{c0}", [P, R, c1 - c0], F32) for c0, c1 in chunks}
         o_w = tile("o_w", [P, S], U32)
         o_s = tile("o_s", [P, S], U8)
         out_rows = out_0.rearrange("(p t) n -> p t n", t=R)
@@ -261,97 +258,92 @@ def tile_picked_twcmxbevo_none_po_kernel(
                 nc.scalar.activation(dst[t][:], win[t][:].indirect(lst[:]), ACT.Exp,
                                      bias=bias[:], scale=tau_c[:, t : t + 1])
 
-        def fetch_product(prod, weight, lst, t, c0, c1, fetched):
-            nc.scalar.activation(fetched, win[t][:].indirect(lst[:, c0 // 16 : c1 // 16]), ACT.Copy)
-            nc.vector.tensor_tensor(prod, weight, fetched, ALU.mult)
-
-        def store_rows(t, c0, c1):
-            nc.sync.dma_start(out_rows[:, t, c0:c1], res[c0][:, t, :])
-
+        QW = S // 4
+        den = [tile(f"den{t}", [P, S], F32) for t in range(R)]
+        den_sq1 = tile("den_sq1", [P, S], F32)
+        den_sq23 = tile("den_sq23", [P, 2, S], F32)
+        den_sq = {1: den_sq1[:], 2: den_sq23[:, 0, :], 3: den_sq23[:, 1, :]}
         inv0 = tile("inv0", [P, S], F32)
-        den = {}
         for t in range(R):
             for h in range(HALVES):
                 cols = slice(HW * h, HW * (h + 1))
-                den[t, h] = tile(f"den{t}_{h}", [P, HW], F32)
-                nc.vector.scalar_tensor_tensor(den[t, h][:], ea[t][:, cols], 0.125, eb[t][:, cols], ALU.add, ALU.add)
+                nc.vector.scalar_tensor_tensor(den[t][:, cols], ea[t][:, cols], 0.125, eb[t][:, cols], ALU.add, ALU.add)
             for h in range(HALVES):
+                cols = slice(HW * h, HW * (h + 1))
                 if t == 0:
-                    nc.vector.reciprocal(inv0[:, HW * h : HW * (h + 1)], den[t, h][:])
+                    nc.vector.reciprocal(inv0[:, cols], den[t][:, cols])
                 else:
-                    nc.vector.tensor_tensor(den_sq[h][:, t - 1, :], den[t, h][:], den[t, h][:], ALU.mult)
-        early = tile("early", [P, 2, S], F32, "exp_bias3")
-        pa0 = tile("pa0", [P, S], F32)
-        pb0 = tile("pb0", [P, S], F32)
-        num0 = tile("num0", [P, S], F32)
-        fetch_product(pa0[:], ea[0][:], n3_l, 0, 0, S, early[:, 0, :])
-        fetch_product(pb0[:], eb[0][:], n4_l, 0, 0, S, early[:, 1, :])
-        nc.vector.tensor_tensor(num0[:], pa0[:], pb0[:], ALU.add)
-        for c0, c1 in chunks:
-            nc.vector.tensor_tensor(res[c0][:, 0, :], num0[:, c0:c1], inv0[:, c0:c1], ALU.mult)
-            store_rows(0, c0, c1)
-        for h in range(HALVES):
-            nc.scalar.activation(inv[h][:], den_sq[h][:], ACT.Abs_reciprocal_sqrt)
+                    nc.vector.tensor_tensor(den_sq[t][:, cols], den[t][:, cols], den[t][:, cols], ALU.mult)
 
-        def finish(c0, c1, res_bf):
-            quantise(o_w[:, c0:c1], o_s[:, c0:c1], res_bf[:])
-            nc.sync.dma_start(out_words[:, c0:c1], o_w[:, c0:c1].bitcast(I32))
+        res = tile("res", [P, 4, R, QW], F32)
+        weight_a, weight_b = list(ea), list(eb)
 
-        fetched = []
-        late = []
-        share_a = tile("share_a", [P, HW], F32)
-        share_b = tile("share_b", [P, HW], F32)
+        def normalise(t, inv):
+            weight_a[t] = tile(f"share_a{t}", [P, S], F32)
+            weight_b[t] = tile(f"share_b{t}", [P, S], F32)
+            nc.vector.tensor_tensor(weight_a[t][:], ea[t][:], inv, ALU.mult)
+            nc.vector.tensor_tensor(weight_b[t][:], eb[t][:], inv, ALU.mult)
 
-        def out_chain(t, c0, c1):
-            h, part = c0 // HW, slice(c0 % HW, c0 % HW + c1 - c0)
-            at_n3 = den_sq[h][:, t - 1, part]
-            at_n4 = (fetched[-2] if len(fetched) > 1 else den[R - 1, len(fetched)][:])[:, : c1 - c0]
-            fetched.append(at_n3)
+        def by_quarters(ap):
+            return ap.rearrange("p (q n) -> p q n", n=QW)
+
+        def out_chain(t, c0, c1, at_n3, at_n4, inv=None):
             pa = tile(f"pa{t}_{c0}", [P, c1 - c0], F32)
             pb = tile(f"pb{t}_{c0}", [P, c1 - c0], F32)
-            if t == R - 1 and h == 1:
 
-                def add_up():
-                    nc.vector.tensor_tensor(res[c0][:, t, :], pa[:], pb[:], ALU.add)
-                    store_rows(t, c0, c1)
+            def fetch_product(prod, weight, lst, fetched):
+                nc.scalar.activation(fetched, win[t][:].indirect(lst[:, c0 // 16 : c1 // 16]), ACT.Copy)
+                nc.vector.tensor_tensor(prod[:], weight[t][:, c0:c1], fetched, ALU.mult)
 
-                res_bf = tile(f"res_bf{c0}", [P, c1 - c0, R], BF16)
-                return [
-                    lambda: fetch_product(pa[:], share_a[:, part], n3_l, t, c0, c1, at_n3),
-                    lambda: fetch_product(pb[:], share_b[:, part], n4_l, t, c0, c1, at_n4),
-                    add_up,
-                    lambda: interleave(res_bf[:], res[c0][:]),
-                    lambda: finish(c0, c1, res_bf),
-                ]
-            num = tile(f"num{t}_{c0}", [P, c1 - c0], F32)
+            def combine(in0, in1, op):
+                nc.vector.tensor_tensor(res[:, c0 // QW : c1 // QW, t, :], by_quarters(in0), by_quarters(in1), op)
+                if c0 == 0 or c1 == S:
+                    s0 = c0 // HW * HW
+                    nc.sync.dma_start(by_quarters(out_rows[:, t, s0:c1]), res[:, s0 // QW : c1 // QW, t, :])
 
-            def divide():
-                for a0, a1 in chunks:
-                    if c0 <= a0 < c1:
-                        nc.vector.tensor_tensor(
-                            res[a0][:, t, :], num[:, a0 - c0 : a1 - c0], inv[h][:, t - 1, a0 - HW * h : a1 - HW * h], ALU.mult)
-                        store_rows(t, a0, a1)
-
-            if t == R - 1:
-                res_bf = tile(f"res_bf{c0}", [P, c1 - c0, R], BF16)
-                late.append(lambda: interleave(res_bf[:], res[c0][:], nc.scalar.copy))
-                late.append(lambda: finish(c0, c1, res_bf))
-            return [
-                lambda: fetch_product(pa[:], ea[t][:, c0:c1], n3_l, t, c0, c1, at_n3),
-                lambda: fetch_product(pb[:], eb[t][:, c0:c1], n4_l, t, c0, c1, at_n4),
+            steps = [
+                lambda: fetch_product(pa, weight_a, n3_l, at_n3),
+                lambda: fetch_product(pb, weight_b, n4_l, at_n4),
+            ]
+            if inv is None:
+                return steps + [lambda: combine(pa[:], pb[:], ALU.add)]
+            num = tile(f"num{t}", [P, S], F32)
+            return steps + [
                 lambda: nc.vector.tensor_tensor(num[:], pa[:], pb[:], ALU.add),
-                divide,
+                lambda: combine(num[:], inv, ALU.mult),
             ]
 
-        nc.vector.tensor_tensor(share_a[:], ea[R - 1][:, HW:], inv[1][:, R - 2, :], ALU.mult)
-        nc.vector.tensor_tensor(share_b[:], eb[R - 1][:, HW:], inv[1][:, R - 2, :], ALU.mult)
-        run_staggered(
-            [out_chain(t, 0, HW) for t in range(1, R)]
-            + [out_chain(t, HW, S) for t in range(1, R - 1)]
-            + [out_chain(R - 1, c0, c1) for c0, c1 in chunks[1:]]
-        )
-        for step in late:
+        res_bf = [tile(f"res_bf{h}", [P, HW, R], BF16) for h in range(HALVES)]
+
+        def finish(h):
+            cols = slice(HW * h, HW * (h + 1))
+            quantise(o_w[:, cols], o_s[:, cols], res_bf[h][:])
+            nc.sync.dma_start(out_words[:, cols], o_w[:, cols].bitcast(I32))
+
+        early = tile("early", [P, 2, S], F32, "exp_bias3")
+        for step in out_chain(0, 0, S, early[:, 0, :], early[:, 1, :], inv0[:]):
             step()
+        inv23 = tile("inv23", [P, 2, S], F32)
+        nc.scalar.activation(inv23[:], den_sq23[:], ACT.Abs_reciprocal_sqrt)
+        inv1 = den_sq[3]
+        nc.scalar.activation(inv1, den_sq[1], ACT.Abs_reciprocal_sqrt)
+        for t in (2, 3):
+            normalise(t, inv23[:, t - 2, :])
+        first = out_chain(1, 0, S, den_sq[1], den[3][:], inv1)
+        for step in first[:3]:
+            step()
+        chains = [[None, None, first[3]], out_chain(2, 0, S, den_sq[2], den_sq[1])]
+        for c0, c1 in chunks:
+            chains.append(out_chain(3, c0, c1, den_sq[2][:, c0:c1], den[3][:, c0:c1]))
+            if c0 >= HW:
+                chains[-1].append(lambda c0=c0, c1=c1: interleave(res_bf[1][:, c0 - HW : c1 - HW, :], res[:, c0 // QW]))
+        run_staggered(chains)
+        nc.scalar.copy(
+            res_bf[0][:].rearrange("p (q c i) t -> p q c t i", q=2, i=4),
+            res[:, :2].rearrange("p q t (c i) -> p q c t i", i=4),
+        )
+        for h in range(HALVES):
+            finish(h)
         for q in range(4):
             queue = nc.scalar if q % 2 else nc.sync
             queue.dma_start(out_scales[4 * q : 4 * q + 4, :], o_s[32 * q : 32 * q + 4, :].bitcast(I32))

@@ -2,8 +2,9 @@ from contextlib import ExitStack
 
 import concourse.mybir as mybir
 
-K, T, S = 512, 2048, 512
-FLOPS = 3 * 2 * 512 * 512 * 512
+T = 2048
+S = 512
+FLOPS = 3 * 2 * S * S * S
 
 F32 = mybir.dt.float32
 BF16 = mybir.dt.bfloat16
@@ -18,9 +19,11 @@ ACT = mybir.ActivationFunctionType
 
 P = 128
 R = 4
-HALVES = 2
-HW = S // HALVES
-HL = HW // 16
+LAST = R - 1
+PER_COL = 16
+HALF = S // 2
+HALVES = ((0, HALF), (HALF, S))
+CHUNKS = ((0, HALF), (HALF, HALF + HALF // 2), (HALF + HALF // 2, S))
 
 
 def tile_picked_twcmxbevo_none_po_kernel(
@@ -29,22 +32,25 @@ def tile_picked_twcmxbevo_none_po_kernel(
 ):
     nc = tc.nc
     with ExitStack() as ctx:
-        sb = ctx.enter_context(tc.tile_pool(name="sb", bufs=1))
-        ps = ctx.enter_context(tc.psum_pool(name="ps", bufs=1))
+        sbuf = ctx.enter_context(tc.tile_pool(name="sbuf", bufs=1))
+        psum = ctx.enter_context(tc.psum_pool(name="psum", bufs=1))
 
-        def tile(name, shape, dtype, tag=None):
-            return sb.tile(shape, dtype, name=name, tag=tag or name, align_bytes=64)
+        def tile(name, shape, dtype, reuse=None):
+            return sbuf.tile(shape, dtype, name=name, tag=reuse or name, align_bytes=64)
+
+        def entries(lst, c0, c1):
+            return lst[:, c0 // PER_COL : c1 // PER_COL]
 
         def load_list(name, src):
-            dst = tile(name, [P, S // 16], U16)
+            dst = tile(name, [P, S // PER_COL], U16)
             nc.sync.dma_start(dst[:], src)
             return dst
 
-        def load_scale_rows(queues, dst, src):
-            for q, queue in enumerate(queues):
-                queue.dma_start(dst[32 * q : 32 * q + 4, :].bitcast(I32), src[0, 4 * q : 4 * q + 4, :].bitcast(I32))
+        def load_scale_rows(dst, src):
+            for q in range(4):
+                nc.sync.dma_start(dst[32 * q : 32 * q + 4, :].bitcast(I32), src[0, 4 * q : 4 * q + 4, :].bitcast(I32))
 
-        def load_column(queue, name, src):
+        def load_per_row(queue, name, src):
             dst = tile(name, [P, R], F32)
             queue.dma_start(dst[:], src.rearrange("(p t) o -> p (t o)", t=R))
             return dst
@@ -59,86 +65,85 @@ def tile_picked_twcmxbevo_none_po_kernel(
         warm = tile("warm", [P, 2], F32)
         nc.gpsimd.memset(warm[:, 0:1], 0.0)
         nc.scalar.activation(warm[:, 1:2], warm[:, 0:1], ACT.Sigmoid)
-        sl_c = load_column(nc.gpsimd, "sl_c", sl)
-        th_c = load_column(nc.gpsimd, "th_c", th)
+
+        sl_r = load_per_row(nc.gpsimd, "sl_r", sl)
+        th_r = load_per_row(nc.gpsimd, "th_r", th)
         two_l = load_list("two_l", two)
         x_w = tile("x_w", [P, T], U32)
         x_src = x_words[0].rearrange("p n t -> p (n t)").bitcast(I32)
         nc.sync.dma_start(x_w[:, : T // 2].bitcast(I32), x_src[:, : T // 2])
-        load_scale_rows([nc.sync] * 4, x_sc, x_scales)
+        load_scale_rows(x_sc, x_scales)
         nc.sync.dma_start(x_w[:, T // 2 :].bitcast(I32), x_src[:, T // 2 :])
         w2_raw = tile("w2_raw", [P, 2 * S], U8)
         nc.sync.dma_start(w2_raw[:].bitcast(I32), w2_words[0].bitcast(I32))
-        load_scale_rows([nc.sync] * 4, w2_sc_raw, w2_scales)
+        load_scale_rows(w2_sc_raw, w2_scales)
         w1_raw = tile("w1_raw", [P, 2 * S], U8)
         nc.sync.dma_start(w1_raw[:].bitcast(I32), w1_words[0].bitcast(I32))
         offs_l = load_list("offs_l", offs)
         n1_l = load_list("n1_l", n1)
         n2_l = load_list("n2_l", n2)
-        load_scale_rows([nc.sync] * 4, w1_sc_raw, w1_scales)
+        load_scale_rows(w1_sc_raw, w1_scales)
         cand_l = load_list("cand_l", cand)
-        gs_c = load_column(nc.sync, "gs_c", gs)
+        gs_r = load_per_row(nc.sync, "gs_r", gs)
         n3_l = load_list("n3_l", n3)
         n4_l = load_list("n4_l", n4)
-        tau_c = load_column(nc.sync, "tau_c", tau)
+        tau_r = load_per_row(nc.sync, "tau_r", tau)
 
-        def gather_scales(name, lst, tag=None):
-            dst = tile(name, [P, S], U8, tag)
+        def gather_scales(name, lst):
+            dst = tile(name, [P, S], U8)
             nc.vector.tensor_copy(dst[:], x_sc[:].indirect(lst[:]))
             return dst
 
-        def gather_words(name, lst, parts=1, tag=None):
-            dst = tile(name, [P, S], U32, tag)
-            for h in range(parts):
-                w = S // parts
-                nc.vector.tensor_copy(dst[:, w * h : w * (h + 1)], x_w[:].indirect(lst[:, w * h // 16 : w * (h + 1) // 16]))
+        def gather_words(name, lst, ranges):
+            dst = tile(name, [P, S], U32)
+            for c0, c1 in ranges:
+                nc.vector.tensor_copy(dst[:, c0:c1], x_w[:].indirect(entries(lst, c0, c1)))
             return dst
 
         def deal(copy, dst, src):
             copy(dst.rearrange("p (t m) -> p t m", t=R), src.rearrange("p (m t) -> p t m", t=R))
 
         def deal_weight(name, raw, sc_raw):
-            w = tile(name, [P, 2 * S], U8)
-            sc = tile(name + "_sc", [P, S], U8)
-            deal(nc.scalar.copy, w[:].bitcast(U16), raw[:].bitcast(U16))
-            deal(nc.vector.tensor_copy, sc[:], sc_raw[:])
-            return w, sc
+            words = tile(name, [P, 2 * S], U8)
+            scales = tile(name + "_sc", [P, S], U8)
+            deal(nc.scalar.copy, words[:].bitcast(U16), raw[:].bitcast(U16))
+            deal(nc.vector.tensor_copy, scales[:], sc_raw[:])
+            return words, scales
 
-        def project(tag, w, sc, xw, xs, parts=1):
-            banks = []
+        def project(banks, w_words, w_scales, picked_words, picked_scales, first_ranges):
+            result = []
             for t in range(R):
-                bank = ps.tile([P, S], F32, name=f"{tag}{t}", tag=f"{tag}{t}")
-                n = S // (parts if t == 0 else 1)
-                for c0 in range(0, S, n):
+                bank = psum.tile([P, S], F32, name=f"{banks}{t}", tag=f"{banks}{t}")
+                for c0, c1 in first_ranges if t == 0 else ((0, S),):
                     nc.tensor.matmul_mx(
-                        out=bank[:, c0 : c0 + n],
-                        lhsT=w[:, 2 * P * t : 2 * P * (t + 1)].bitcast(FP4X4),
-                        lhsT_scale=sc[:, P * t : P * (t + 1)],
-                        rhs=xw[:, c0 : c0 + n].bitcast(FP8X4),
-                        rhs_scale=xs[:, c0 : c0 + n],
+                        out=bank[:, c0:c1],
+                        lhsT=w_words[:, 2 * P * t : 2 * P * (t + 1)].bitcast(FP4X4),
+                        lhsT_scale=w_scales[:, P * t : P * (t + 1)],
+                        rhs=picked_words[:, c0:c1].bitcast(FP8X4),
+                        rhs_scale=picked_scales[:, c0:c1],
                         start=True,
                         stop=True,
                     )
-                banks.append(bank)
-            return banks
+                result.append(bank)
+            return result
 
         two_s = gather_scales("two_s", two_l)
         two_w = gather_words("two_w", two_l, HALVES)
         w2, w2_sc = deal_weight("w2", w2_raw, w2_sc_raw)
-        d_ps = project("a", w2, w2_sc, two_w, two_s, HALVES)
+        d_ps = project("bank_d", w2, w2_sc, two_w, two_s, HALVES)
 
         sig_bias = tile("sig_bias", [P, R], F32)
         sl_th = tile("sl_th", [P, R], F32)
-        nc.gpsimd.tensor_tensor(sl_th[:], sl_c[:], th_c[:], ALU.mult)
+        nc.gpsimd.tensor_tensor(sl_th[:], sl_r[:], th_r[:], ALU.mult)
         nc.gpsimd.tensor_scalar(sig_bias[:], sl_th[:], -1.0, 0.0, ALU.mult, ALU.add)
 
         offs_s = gather_scales("offs_s", offs_l)
-        offs_w = gather_words("offs_w", offs_l)
+        offs_w = gather_words("offs_w", offs_l, ((0, S),))
         w1, w1_sc = deal_weight("w1", w1_raw, w1_sc_raw)
-        y_ps = project("b", w1, w1_sc, offs_w, offs_s)
+        y_ps = project("bank_y", w1, w1_sc, offs_w, offs_s, ((0, S),))
 
         cand_s_raw = gather_scales("cand_s_raw", cand_l)
-        cand_w_raw = gather_words("cand_w_raw", cand_l)
+        cand_w_raw = gather_words("cand_w_raw", cand_l, ((0, S),))
         cand_s = tile("cand_s", [P, S], U8)
         cand_w = tile("cand_w", [P, S], U32)
         deal(nc.vector.tensor_copy, cand_s[:], cand_s_raw[:])
@@ -146,86 +151,76 @@ def tile_picked_twcmxbevo_none_po_kernel(
             cand_w[:].rearrange("p (t m) -> p m t", t=R), cand_w_raw[:].rearrange("p (m t) -> p m t", t=R)
         )
 
-        def interleave(dst, src, copy=nc.vector.tensor_copy):
-            copy(
-                dst.rearrange("p (c i) t -> p c t i", i=4), src.rearrange("p t (c i) -> p c t i", i=4)
-            )
+        def interleave(copy, dst, src):
+            copy(dst.rearrange("p (c i) t -> p c t i", i=4), src.rearrange("p t (c i) -> p c t i", i=4))
 
         def quantise(words, scales, src):
             nc.vector.quantize_mx(out=words.bitcast(FP8X4), scales=scales, in_=src.rearrange("p n t -> p (n t)"))
 
         def run_staggered(chains):
-            for step in range(len(chains) + 2):
+            for round_no in range(len(chains) + 2):
                 for stage in (0, 2, 4, 1, 3, 5):
-                    i = step - stage // 2
+                    i = round_no - stage // 2
                     if 0 <= i < len(chains) and stage < len(chains[i]) and chains[i][stage]:
                         chains[i][stage]()
 
-        full = (slice(0, S), slice(0, S // 16))
-        halves = [(slice(HW * h, HW * (h + 1)), slice(HL * h, HL * (h + 1))) for h in range(HALVES)]
-
         z_w = tile("z_w", [P, S], U32)
         z_s = tile("z_s", [P, S], U8)
-        chunks = ((0, 256), (256, 384), (384, 512))
-        z_planes = {c0: tile(f"z_planes{c0}", [P, R, c1 - c0], BF16) for c0, c1 in chunks}
+        z_rows = {c0: tile(f"z_rows{c0}", [P, R, c1 - c0], BF16) for c0, c1 in CHUNKS}
         d_sb = [tile(f"d_sb{t}", [P, S], F32) for t in range(R)]
-        win = [tile(f"win{t}", [P, 2 * S], F32) for t in range(R)]
-
+        s_win = [tile(f"s_win{t}", [P, 2 * S], F32) for t in range(R)]
         sg_tiles = []
 
         def z_chain(t, c0, c1):
-            cols, lcols = slice(c0, c1), slice(c0 // 16, c1 // 16)
-            gated = win[t][:, S + c0 : S + c1]
-            last = t == R - 1
+            gated = s_win[t][:, S + c0 : S + c1]
             sg = tile(f"sg{t}_{c0}", [P, c1 - c0], F32)
-            far = tile(f"far{t}_{c0}", [P, c1 - c0], F32)
-            diff = sg_tiles[-1][:, : c1 - c0] if sg_tiles else tile("diff_first", [P, c1 - c0], F32, "cand_w_raw")[:]
+            d_n2 = tile(f"d_n2_{t}_{c0}", [P, c1 - c0], F32)
+            if sg_tiles:
+                diff = sg_tiles[-1][:, : c1 - c0]
+            else:
+                diff = tile("diff_first", [P, c1 - c0], F32, "cand_w_raw")[:]
             sg_tiles.append(sg)
-            big = tile(f"big{t}_{c0}", [P, c1 - c0], F32)
+            larger = tile(f"larger{t}_{c0}", [P, c1 - c0], F32)
 
             def gate():
                 if c0 == 0:
                     nc.scalar.copy(d_sb[t][:], d_ps[t][:])
-                nc.scalar.activation(sg[:], d_sb[t][:].indirect(n1_l[:, lcols]), ACT.Sigmoid,
-                                     bias=sig_bias[:, t : t + 1], scale=sl_c[:, t : t + 1])
-                nc.vector.tensor_tensor(gated, y_ps[t][:, cols], sg[:], ALU.mult)
+                nc.scalar.activation(sg[:], d_sb[t][:].indirect(entries(n1_l, c0, c1)), ACT.Sigmoid,
+                                     bias=sig_bias[:, t : t + 1], scale=sl_r[:, t : t + 1])
+                nc.vector.tensor_tensor(gated, y_ps[t][:, c0:c1], sg[:], ALU.mult)
 
-            def differ():
-                nc.scalar.activation(far[:], d_sb[t][:].indirect(n2_l[:, lcols]), ACT.Copy)
-                nc.vector.tensor_tensor(diff, far[:], d_ps[t][:, cols], ALU.subtract)
+            def subtract():
+                nc.scalar.activation(d_n2[:], d_sb[t][:].indirect(entries(n2_l, c0, c1)), ACT.Copy)
+                nc.vector.tensor_tensor(diff, d_n2[:], d_ps[t][:, c0:c1], ALU.subtract)
 
             def weigh():
-                for a0, a1 in chunks:
+                engine = nc.vector if t == LAST else nc.gpsimd
+                for a0, a1 in CHUNKS:
                     if c0 <= a0 < c1:
-                        (nc.vector if last else nc.gpsimd).tensor_scalar(
-                            z_planes[a0][:, t, :], big[:, a0 - c0 : a1 - c0], gs_c[:, t : t + 1], 0.0, ALU.mult, ALU.add)
+                        engine.tensor_scalar(z_rows[a0][:, t, :], larger[:, a0 - c0 : a1 - c0],
+                                             gs_r[:, t : t + 1], 0.0, ALU.mult, ALU.add)
 
-            steps = [gate, differ, lambda: nc.vector.tensor_tensor(big[:], gated, diff, ALU.max), weigh]
-            if last:
+            stages = [gate, subtract, lambda: nc.vector.tensor_tensor(larger[:], gated, diff, ALU.max), weigh]
+            if t == LAST:
                 z_bf = tile(f"z_bf{c0}", [P, c1 - c0, R], BF16)
-                steps.append(lambda: interleave(z_bf[:], z_planes[c0][:]))
-                steps.append(lambda: quantise(z_w[:, cols], z_s[:, cols], z_bf[:]))
-            return steps
+                stages.append(lambda: interleave(nc.vector.tensor_copy, z_bf[:], z_rows[c0][:]))
+                stages.append(lambda: quantise(z_w[:, c0:c1], z_s[:, c0:c1], z_bf[:]))
+            return stages
 
         run_staggered(
-            [z_chain(t, 0, HW) for t in range(R)]
-            + [z_chain(t, HW, S) for t in range(R - 1)]
-            + [z_chain(R - 1, c0, c1) for c0, c1 in chunks[1:]]
+            [z_chain(t, 0, HALF) for t in range(R)]
+            + [z_chain(t, HALF, S) for t in range(LAST)]
+            + [z_chain(LAST, c0, c1) for c0, c1 in CHUNKS[1:]]
         )
 
         neg_tau = tile("neg_tau", [P, R], F32)
-        nc.gpsimd.tensor_scalar(neg_tau[:], tau_c[:], -1.0, 0.0, ALU.mult, ALU.add)
+        nc.gpsimd.tensor_scalar(neg_tau[:], tau_r[:], -1.0, 0.0, ALU.mult, ALU.add)
         ea = [tile(f"ea{t}", [P, S], F32) for t in range(R)]
-        eb = [tile(f"eb{t}", [P, S], F32) for t in range(R)]
-        o_w = tile("o_w", [P, S], U32)
-        o_s = tile("o_s", [P, S], U8)
-        out_rows = out_0.rearrange("(p t) n -> p t n", t=R)
-        out_words = out_1[0].rearrange("p n t -> p (n t)").bitcast(I32)
-        out_scales = out_2[0].bitcast(I32)
+        ea2 = [tile(f"ea2_{t}", [P, S], F32) for t in range(R)]
 
         def score(t, bank, c0, c1):
             nc.tensor.matmul_mx(
-                out=bank,
+                out=bank[:, c0:c1],
                 lhsT=cand_w[:, P * t : P * (t + 1)].bitcast(FP8X4),
                 lhsT_scale=cand_s[:, P * t : P * (t + 1)],
                 rhs=z_w[:, c0:c1].bitcast(FP8X4),
@@ -234,116 +229,119 @@ def tile_picked_twcmxbevo_none_po_kernel(
                 stop=True,
             )
 
-        def leave_psum(name, t, bank, c0, c1):
-            top = tile(name, [P, 1], F32)
-            nc.vector.tensor_scalar(win[t][:, c0:c1], bank, 0.0625, None, ALU.mult, ALU.max, accum_out=top[:])
+        def leave_psum(t, bank, c0, c1, reuse=None):
+            top = tile(f"top{t}_{c0}", [P, 1], F32, reuse)
+            nc.vector.tensor_scalar(s_win[t][:, c0:c1], bank[:, c0:c1], 0.0625, None, ALU.mult, ALU.max,
+                                    accum_out=top[:])
             return top
 
         for t in range(R):
-            bank = ps.tile([P, S], F32, name=f"s{t}", tag=f"a{t}")
-            bias = tile(f"exp_bias{t}", [P, 1], F32)
+            bank = psum.tile([P, S], F32, name=f"bank_s{t}", tag=f"bank_d{t}")
+            exp_bias = tile(f"exp_bias{t}", [P, 1], F32)
             if t == 0:
-                side = ps.tile([P, S], F32, name="s0_side", tag="b0")
-                score(t, side[:, :HW], 0, HW)
-                top_a = leave_psum("top0a", t, side[:, :HW], 0, HW)
-                for c0, c1 in chunks[1:]:
-                    score(t, bank[:, c0:c1], c0, c1)
-                top_b = leave_psum("top0b", t, bank[:, HW:], HW, S)
-                nc.vector.tensor_scalar(bias[:], top_b[:], top_a[:], neg_tau[:, t : t + 1], ALU.max, ALU.mult)
+                side = psum.tile([P, S], F32, name="bank_s0_side", tag="bank_y0")
+                score(t, side, 0, HALF)
+                top_lo = leave_psum(t, side, 0, HALF)
+                for c0, c1 in CHUNKS[1:]:
+                    score(t, bank, c0, c1)
+                top_hi = leave_psum(t, bank, HALF, S, "top")
+                nc.vector.tensor_scalar(exp_bias[:], top_hi[:], top_lo[:], neg_tau[:, t : t + 1], ALU.max, ALU.mult)
             else:
-                score(t, bank[:], 0, S)
-                top = leave_psum(f"top{t}", t, bank[:], 0, S)
-                nc.vector.tensor_tensor(bias[:], top[:], neg_tau[:, t : t + 1], ALU.mult)
-            for dst, lst in ((ea, n3_l), (eb, n4_l)):
-                nc.scalar.activation(dst[t][:], win[t][:].indirect(lst[:]), ACT.Exp,
-                                     bias=bias[:], scale=tau_c[:, t : t + 1])
+                score(t, bank, 0, S)
+                top = leave_psum(t, bank, 0, S, "top")
+                nc.vector.tensor_tensor(exp_bias[:], top[:], neg_tau[:, t : t + 1], ALU.mult)
+            for dst, lst in ((ea, n3_l), (ea2, n4_l)):
+                nc.scalar.activation(dst[t][:], s_win[t][:].indirect(lst[:]), ACT.Exp,
+                                     bias=exp_bias[:], scale=tau_r[:, t : t + 1])
 
-        QW = S // 4
-        den = [tile(f"den{t}", [P, S], F32) for t in range(R)]
+        den = [tile(f"den{t}", [P, S], F32, "top" if t == 0 else None) for t in range(R)]
         den_sq1 = tile("den_sq1", [P, S], F32)
         den_sq23 = tile("den_sq23", [P, 2, S], F32)
         den_sq = {1: den_sq1[:], 2: den_sq23[:, 0, :], 3: den_sq23[:, 1, :]}
         inv0 = tile("inv0", [P, S], F32)
         for t in range(R):
-            for h in range(HALVES):
-                cols = slice(HW * h, HW * (h + 1))
-                nc.vector.scalar_tensor_tensor(den[t][:, cols], ea[t][:, cols], 0.125, eb[t][:, cols], ALU.add, ALU.add)
-            for h in range(HALVES):
-                cols = slice(HW * h, HW * (h + 1))
+            for c0, c1 in HALVES:
+                nc.vector.scalar_tensor_tensor(den[t][:, c0:c1], ea[t][:, c0:c1], 0.125, ea2[t][:, c0:c1],
+                                               ALU.add, ALU.add)
+            for c0, c1 in HALVES:
                 if t == 0:
-                    nc.vector.reciprocal(inv0[:, cols], den[t][:, cols])
+                    nc.vector.reciprocal(inv0[:, c0:c1], den[t][:, c0:c1])
                 else:
-                    nc.vector.tensor_tensor(den_sq[t][:, cols], den[t][:, cols], den[t][:, cols], ALU.mult)
+                    nc.vector.tensor_tensor(den_sq[t][:, c0:c1], den[t][:, c0:c1], den[t][:, c0:c1], ALU.mult)
 
-        res = tile("res", [P, 4, R, QW], F32)
-        weight_a, weight_b = list(ea), list(eb)
+        res = [tile(f"res{c0}", [P, R, HALF], F32) for c0, c1 in HALVES]
+        res_bf = [tile(f"res_bf{c0}", [P, HALF, R], BF16) for c0, c1 in HALVES]
+        out_w = tile("out_w", [P, S], U32)
+        out_s = tile("out_s", [P, S], U8)
+        out_rows = out_0.rearrange("(p t) n -> p t n", t=R)
+        out_words = out_1[0].rearrange("p n t -> p (n t)").bitcast(I32)
+        out_scales = out_2[0].bitcast(I32)
 
-        def normalise(t, inv):
-            weight_a[t] = tile(f"share_a{t}", [P, S], F32)
-            weight_b[t] = tile(f"share_b{t}", [P, S], F32)
-            nc.vector.tensor_tensor(weight_a[t][:], ea[t][:], inv, ALU.mult)
-            nc.vector.tensor_tensor(weight_b[t][:], eb[t][:], inv, ALU.mult)
+        def normalised(t, inv):
+            share = tile(f"share{t}", [P, S], F32)
+            share2 = tile(f"share2_{t}", [P, S], F32)
+            nc.vector.tensor_tensor(share[:], ea[t][:], inv, ALU.mult)
+            nc.vector.tensor_tensor(share2[:], ea2[t][:], inv, ALU.mult)
+            return share, share2
 
-        def by_quarters(ap):
-            return ap.rearrange("p (q n) -> p q n", n=QW)
+        def out_chain(t, c0, c1, weights, s_n3, s_n4, inv=None):
+            prod = tile(f"prod{t}_{c0}", [P, c1 - c0], F32)
+            prod2 = tile(f"prod2_{t}_{c0}", [P, c1 - c0], F32)
 
-        def out_chain(t, c0, c1, at_n3, at_n4, inv=None):
-            pa = tile(f"pa{t}_{c0}", [P, c1 - c0], F32)
-            pb = tile(f"pb{t}_{c0}", [P, c1 - c0], F32)
-
-            def fetch_product(prod, weight, lst, fetched):
-                nc.scalar.activation(fetched, win[t][:].indirect(lst[:, c0 // 16 : c1 // 16]), ACT.Copy)
-                nc.vector.tensor_tensor(prod[:], weight[t][:, c0:c1], fetched, ALU.mult)
+            def fetch_product(dst, weight, lst, fetched):
+                nc.scalar.activation(fetched, s_win[t][:].indirect(entries(lst, c0, c1)), ACT.Copy)
+                nc.vector.tensor_tensor(dst[:], weight[:, c0:c1], fetched, ALU.mult)
 
             def combine(in0, in1, op):
-                nc.vector.tensor_tensor(res[:, c0 // QW : c1 // QW, t, :], by_quarters(in0), by_quarters(in1), op)
-                if c0 == 0 or c1 == S:
-                    s0 = c0 // HW * HW
-                    nc.sync.dma_start(by_quarters(out_rows[:, t, s0:c1]), res[:, s0 // QW : c1 // QW, t, :])
+                for h, (h0, h1) in enumerate(HALVES):
+                    lo, hi = max(c0, h0), min(c1, h1)
+                    if lo < hi:
+                        nc.vector.tensor_tensor(res[h][:, t, lo - h0 : hi - h0], in0[:, lo - c0 : hi - c0],
+                                                in1[:, lo - c0 : hi - c0], op)
+                        if hi == h1:
+                            nc.sync.dma_start(out_rows[:, t, h0:h1], res[h][:, t, :])
 
-            steps = [
-                lambda: fetch_product(pa, weight_a, n3_l, at_n3),
-                lambda: fetch_product(pb, weight_b, n4_l, at_n4),
+            stages = [
+                lambda: fetch_product(prod, weights[0], n3_l, s_n3),
+                lambda: fetch_product(prod2, weights[1], n4_l, s_n4),
             ]
             if inv is None:
-                return steps + [lambda: combine(pa[:], pb[:], ALU.add)]
+                return stages + [lambda: combine(prod, prod2, ALU.add)]
             num = tile(f"num{t}", [P, S], F32)
-            return steps + [
-                lambda: nc.vector.tensor_tensor(num[:], pa[:], pb[:], ALU.add),
-                lambda: combine(num[:], inv, ALU.mult),
+            return stages + [
+                lambda: nc.vector.tensor_tensor(num[:], prod[:], prod2[:], ALU.add),
+                lambda: combine(num, inv, ALU.mult),
             ]
 
-        res_bf = [tile(f"res_bf{h}", [P, HW, R], BF16) for h in range(HALVES)]
-
-        def finish(h):
-            cols = slice(HW * h, HW * (h + 1))
-            quantise(o_w[:, cols], o_s[:, cols], res_bf[h][:])
-            nc.sync.dma_start(out_words[:, cols], o_w[:, cols].bitcast(I32))
-
-        early = tile("early", [P, 2, S], F32, "exp_bias3")
-        for step in out_chain(0, 0, S, early[:, 0, :], early[:, 1, :], inv0[:]):
-            step()
+        s0_fetched = tile("s0_fetched", [P, 2, S], F32, f"exp_bias{LAST}")
+        for stage_call in out_chain(0, 0, S, (ea[0], ea2[0]), s0_fetched[:, 0, :], s0_fetched[:, 1, :], inv0):
+            stage_call()
         inv23 = tile("inv23", [P, 2, S], F32)
         nc.scalar.activation(inv23[:], den_sq23[:], ACT.Abs_reciprocal_sqrt)
         inv1 = den_sq[3]
         nc.scalar.activation(inv1, den_sq[1], ACT.Abs_reciprocal_sqrt)
-        for t in (2, 3):
-            normalise(t, inv23[:, t - 2, :])
-        first = out_chain(1, 0, S, den_sq[1], den[3][:], inv1)
-        for step in first[:3]:
-            step()
-        chains = [[None, None, first[3]], out_chain(2, 0, S, den_sq[2], den_sq[1])]
-        for c0, c1 in chunks:
-            chains.append(out_chain(3, c0, c1, den_sq[2][:, c0:c1], den[3][:, c0:c1]))
-            if c0 >= HW:
-                chains[-1].append(lambda c0=c0, c1=c1: interleave(res_bf[1][:, c0 - HW : c1 - HW, :], res[:, c0 // QW]))
+        shares = {t: normalised(t, inv23[:, t - 2, :]) for t in (2, 3)}
+
+        tile1 = out_chain(1, 0, S, (ea[1], ea2[1]), den_sq[1], den[3][:], inv1)
+        for stage_call in tile1[:3]:
+            stage_call()
+        chains = [
+            [None, None, tile1[3]],
+            out_chain(2, 0, HALF, shares[2], den_sq[2][:, :HALF], den_sq[1][:, :HALF]),
+            out_chain(3, 0, HALF, shares[3], den_sq[2][:, HALF:], den[3][:, :HALF]),
+            out_chain(2, HALF, S, shares[2], den_sq[1][:, HALF:], den[3][:, HALF:]),
+        ]
+        for c0, c1 in CHUNKS[1:]:
+            quarter = slice(c0 - HALF, c1 - HALF)
+            chains.append(out_chain(3, c0, c1, shares[3], den_sq[2][:, quarter], den_sq[1][:, quarter]))
+            chains[-1].append(
+                lambda cols=quarter: interleave(nc.vector.tensor_copy, res_bf[1][:, cols, :], res[1][:, :, cols])
+            )
         run_staggered(chains)
-        nc.scalar.copy(
-            res_bf[0][:].rearrange("p (q c i) t -> p q c t i", q=2, i=4),
-            res[:, :2].rearrange("p q t (c i) -> p q c t i", i=4),
-        )
-        for h in range(HALVES):
-            finish(h)
+        interleave(nc.scalar.copy, res_bf[0][:], res[0][:])
+        for h, (c0, c1) in enumerate(HALVES):
+            quantise(out_w[:, c0:c1], out_s[:, c0:c1], res_bf[h][:])
+            nc.sync.dma_start(out_words[:, c0:c1], out_w[:, c0:c1].bitcast(I32))
         for q in range(4):
             queue = nc.scalar if q % 2 else nc.sync
-            queue.dma_start(out_scales[4 * q : 4 * q + 4, :], o_s[32 * q : 32 * q + 4, :].bitcast(I32))
+            queue.dma_start(out_scales[4 * q : 4 * q + 4, :], out_s[32 * q : 32 * q + 4, :].bitcast(I32))

from contextlib import ExitStack

import concourse.mybir as mybir

T = 2048
S = 512
FLOPS = 3 * 2 * S * S * S

F32 = mybir.dt.float32
BF16 = mybir.dt.bfloat16
I32 = mybir.dt.int32
U32 = mybir.dt.uint32
U16 = mybir.dt.uint16
U8 = mybir.dt.uint8
FP8X4 = mybir.dt.float8_e4m3fn_x4
FP4X4 = mybir.dt.float4_e2m1fn_x4
ALU = mybir.AluOpType
ACT = mybir.ActivationFunctionType

P = 128
R = 4
LAST = R - 1
PER_COL = 16
HALF = S // 2
HALVES = ((0, HALF), (HALF, S))
CHUNKS = ((0, HALF), (HALF, HALF + HALF // 2), (HALF + HALF // 2, S))


def tile_picked_twcmxbevo_none_po_kernel(
    tc, x_words, x_scales, w1_words, w1_scales, w2_words, w2_scales, sl, th, gs, tau,
    offs, two, n1, n2, cand, n3, n4, out_0, out_1, out_2,
):
    nc = tc.nc
    with ExitStack() as ctx:
        sbuf = ctx.enter_context(tc.tile_pool(name="sbuf", bufs=1))
        psum = ctx.enter_context(tc.psum_pool(name="psum", bufs=1))

        def tile(name, shape, dtype, reuse=None):
            return sbuf.tile(shape, dtype, name=name, tag=reuse or name, align_bytes=64)

        def entries(lst, c0, c1):
            return lst[:, c0 // PER_COL : c1 // PER_COL]

        def load_list(name, src):
            dst = tile(name, [P, S // PER_COL], U16)
            nc.sync.dma_start(dst[:], src)
            return dst

        def load_scale_rows(dst, src):
            for q in range(4):
                nc.sync.dma_start(dst[32 * q : 32 * q + 4, :].bitcast(I32), src[0, 4 * q : 4 * q + 4, :].bitcast(I32))

        def load_per_row(queue, name, src):
            dst = tile(name, [P, R], F32)
            queue.dma_start(dst[:], src.rearrange("(p t) o -> p (t o)", t=R))
            return dst

        x_sc = tile("x_sc", [P, T], U8)
        w2_sc_raw = tile("w2_sc_raw", [P, S], U8)
        w1_sc_raw = tile("w1_sc_raw", [P, S], U8)
        nc.vector.memset(x_sc[:].bitcast(I32), 0)
        nc.vector.memset(w2_sc_raw[:].bitcast(I32), 0)
        nc.vector.memset(w1_sc_raw[:].bitcast(I32), 0)

        warm = tile("warm", [P, 2], F32)
        nc.gpsimd.memset(warm[:, 0:1], 0.0)
        nc.scalar.activation(warm[:, 1:2], warm[:, 0:1], ACT.Sigmoid)

        sl_r = load_per_row(nc.gpsimd, "sl_r", sl)
        th_r = load_per_row(nc.gpsimd, "th_r", th)
        two_l = load_list("two_l", two)
        x_w = tile("x_w", [P, T], U32)
        x_src = x_words[0].rearrange("p n t -> p (n t)").bitcast(I32)
        nc.sync.dma_start(x_w[:, : T // 2].bitcast(I32), x_src[:, : T // 2])
        load_scale_rows(x_sc, x_scales)
        nc.sync.dma_start(x_w[:, T // 2 :].bitcast(I32), x_src[:, T // 2 :])
        w2_raw = tile("w2_raw", [P, 2 * S], U8)
        nc.sync.dma_start(w2_raw[:].bitcast(I32), w2_words[0].bitcast(I32))
        load_scale_rows(w2_sc_raw, w2_scales)
        w1_raw = tile("w1_raw", [P, 2 * S], U8)
        nc.sync.dma_start(w1_raw[:].bitcast(I32), w1_words[0].bitcast(I32))
        offs_l = load_list("offs_l", offs)
        n1_l = load_list("n1_l", n1)
        n2_l = load_list("n2_l", n2)
        load_scale_rows(w1_sc_raw, w1_scales)
        cand_l = load_list("cand_l", cand)
        gs_r = load_per_row(nc.sync, "gs_r", gs)
        n3_l = load_list("n3_l", n3)
        n4_l = load_list("n4_l", n4)
        tau_r = load_per_row(nc.sync, "tau_r", tau)

        def gather_scales(name, lst):
            dst = tile(name, [P, S], U8)
            nc.vector.tensor_copy(dst[:], x_sc[:].indirect(lst[:]))
            return dst

        def gather_words(name, lst, ranges):
            dst = tile(name, [P, S], U32)
            for c0, c1 in ranges:
                nc.vector.tensor_copy(dst[:, c0:c1], x_w[:].indirect(entries(lst, c0, c1)))
            return dst

        def deal(copy, dst, src):
            copy(dst.rearrange("p (t m) -> p t m", t=R), src.rearrange("p (m t) -> p t m", t=R))

        def deal_weight(name, raw, sc_raw):
            words = tile(name, [P, 2 * S], U8)
            scales = tile(name + "_sc", [P, S], U8)
            deal(nc.scalar.copy, words[:].bitcast(U16), raw[:].bitcast(U16))
            deal(nc.vector.tensor_copy, scales[:], sc_raw[:])
            return words, scales

        def project(banks, w_words, w_scales, picked_words, picked_scales, first_ranges):
            result = []
            for t in range(R):
                bank = psum.tile([P, S], F32, name=f"{banks}{t}", tag=f"{banks}{t}")
                for c0, c1 in first_ranges if t == 0 else ((0, S),):
                    nc.tensor.matmul_mx(
                        out=bank[:, c0:c1],
                        lhsT=w_words[:, 2 * P * t : 2 * P * (t + 1)].bitcast(FP4X4),
                        lhsT_scale=w_scales[:, P * t : P * (t + 1)],
                        rhs=picked_words[:, c0:c1].bitcast(FP8X4),
                        rhs_scale=picked_scales[:, c0:c1],
                        start=True,
                        stop=True,
                    )
                result.append(bank)
            return result

        two_s = gather_scales("two_s", two_l)
        two_w = gather_words("two_w", two_l, HALVES)
        w2, w2_sc = deal_weight("w2", w2_raw, w2_sc_raw)
        d_ps = project("bank_d", w2, w2_sc, two_w, two_s, HALVES)

        sig_bias = tile("sig_bias", [P, R], F32)
        sl_th = tile("sl_th", [P, R], F32)
        nc.gpsimd.tensor_tensor(sl_th[:], sl_r[:], th_r[:], ALU.mult)
        nc.gpsimd.tensor_scalar(sig_bias[:], sl_th[:], -1.0, 0.0, ALU.mult, ALU.add)

        offs_s = gather_scales("offs_s", offs_l)
        offs_w = gather_words("offs_w", offs_l, ((0, S),))
        w1, w1_sc = deal_weight("w1", w1_raw, w1_sc_raw)
        y_ps = project("bank_y", w1, w1_sc, offs_w, offs_s, ((0, S),))

        cand_s_raw = gather_scales("cand_s_raw", cand_l)
        cand_w_raw = gather_words("cand_w_raw", cand_l, ((0, S),))
        cand_s = tile("cand_s", [P, S], U8)
        cand_w = tile("cand_w", [P, S], U32)
        deal(nc.vector.tensor_copy, cand_s[:], cand_s_raw[:])
        nc.vector.tensor_copy(
            cand_w[:].rearrange("p (t m) -> p m t", t=R), cand_w_raw[:].rearrange("p (m t) -> p m t", t=R)
        )

        def interleave(copy, dst, src):
            copy(dst.rearrange("p (c i) t -> p c t i", i=4), src.rearrange("p t (c i) -> p c t i", i=4))

        def quantise(words, scales, src):
            nc.vector.quantize_mx(out=words.bitcast(FP8X4), scales=scales, in_=src.rearrange("p n t -> p (n t)"))

        def run_staggered(chains):
            for round_no in range(len(chains) + 2):
                for stage in (0, 2, 4, 1, 3, 5):
                    i = round_no - stage // 2
                    if 0 <= i < len(chains) and stage < len(chains[i]) and chains[i][stage]:
                        chains[i][stage]()

        z_w = tile("z_w", [P, S], U32)
        z_s = tile("z_s", [P, S], U8)
        z_rows = {c0: tile(f"z_rows{c0}", [P, R, c1 - c0], BF16) for c0, c1 in CHUNKS}
        d_sb = [tile(f"d_sb{t}", [P, S], F32) for t in range(R)]
        s_win = [tile(f"s_win{t}", [P, 2 * S], F32) for t in range(R)]
        sg_tiles = []

        def z_chain(t, c0, c1):
            gated = s_win[t][:, S + c0 : S + c1]
            sg = tile(f"sg{t}_{c0}", [P, c1 - c0], F32)
            d_n2 = tile(f"d_n2_{t}_{c0}", [P, c1 - c0], F32)
            if sg_tiles:
                diff = sg_tiles[-1][:, : c1 - c0]
            else:
                diff = tile("diff_first", [P, c1 - c0], F32, "cand_w_raw")[:]
            sg_tiles.append(sg)
            larger = tile(f"larger{t}_{c0}", [P, c1 - c0], F32)

            def gate():
                if c0 == 0:
                    nc.scalar.copy(d_sb[t][:], d_ps[t][:])
                nc.scalar.activation(sg[:], d_sb[t][:].indirect(entries(n1_l, c0, c1)), ACT.Sigmoid,
                                     bias=sig_bias[:, t : t + 1], scale=sl_r[:, t : t + 1])
                nc.vector.tensor_tensor(gated, y_ps[t][:, c0:c1], sg[:], ALU.mult)

            def subtract():
                nc.scalar.activation(d_n2[:], d_sb[t][:].indirect(entries(n2_l, c0, c1)), ACT.Copy)
                nc.vector.tensor_tensor(diff, d_n2[:], d_ps[t][:, c0:c1], ALU.subtract)

            def weigh():
                engine = nc.vector if t == LAST else nc.gpsimd
                for a0, a1 in CHUNKS:
                    if c0 <= a0 < c1:
                        engine.tensor_scalar(z_rows[a0][:, t, :], larger[:, a0 - c0 : a1 - c0],
                                             gs_r[:, t : t + 1], 0.0, ALU.mult, ALU.add)

            stages = [gate, subtract, lambda: nc.vector.tensor_tensor(larger[:], gated, diff, ALU.max), weigh]
            if t == LAST:
                z_bf = tile(f"z_bf{c0}", [P, c1 - c0, R], BF16)
                stages.append(lambda: interleave(nc.vector.tensor_copy, z_bf[:], z_rows[c0][:]))
                stages.append(lambda: quantise(z_w[:, c0:c1], z_s[:, c0:c1], z_bf[:]))
            return stages

        run_staggered(
            [z_chain(t, 0, HALF) for t in range(R)]
            + [z_chain(t, HALF, S) for t in range(LAST)]
            + [z_chain(LAST, c0, c1) for c0, c1 in CHUNKS[1:]]
        )

        neg_tau = tile("neg_tau", [P, R], F32)
        nc.gpsimd.tensor_scalar(neg_tau[:], tau_r[:], -1.0, 0.0, ALU.mult, ALU.add)
        ea = [tile(f"ea{t}", [P, S], F32) for t in range(R)]
        ea2 = [tile(f"ea2_{t}", [P, S], F32) for t in range(R)]

        def score(t, bank, c0, c1):
            nc.tensor.matmul_mx(
                out=bank[:, c0:c1],
                lhsT=cand_w[:, P * t : P * (t + 1)].bitcast(FP8X4),
                lhsT_scale=cand_s[:, P * t : P * (t + 1)],
                rhs=z_w[:, c0:c1].bitcast(FP8X4),
                rhs_scale=z_s[:, c0:c1],
                start=True,
                stop=True,
            )

        def leave_psum(t, bank, c0, c1, reuse=None):
            top = tile(f"top{t}_{c0}", [P, 1], F32, reuse)
            nc.vector.tensor_scalar(s_win[t][:, c0:c1], bank[:, c0:c1], 0.0625, None, ALU.mult, ALU.max,
                                    accum_out=top[:])
            return top

        for t in range(R):
            bank = psum.tile([P, S], F32, name=f"bank_s{t}", tag=f"bank_d{t}")
            exp_bias = tile(f"exp_bias{t}", [P, 1], F32)
            if t == 0:
                side = psum.tile([P, S], F32, name="bank_s0_side", tag="bank_y0")
                score(t, side, 0, HALF)
                top_lo = leave_psum(t, side, 0, HALF)
                for c0, c1 in CHUNKS[1:]:
                    score(t, bank, c0, c1)
                top_hi = leave_psum(t, bank, HALF, S, "top")
                nc.vector.tensor_scalar(exp_bias[:], top_hi[:], top_lo[:], neg_tau[:, t : t + 1], ALU.max, ALU.mult)
            else:
                score(t, bank, 0, S)
                top = leave_psum(t, bank, 0, S, "top")
                nc.vector.tensor_tensor(exp_bias[:], top[:], neg_tau[:, t : t + 1], ALU.mult)
            for dst, lst in ((ea, n3_l), (ea2, n4_l)):
                nc.scalar.activation(dst[t][:], s_win[t][:].indirect(lst[:]), ACT.Exp,
                                     bias=exp_bias[:], scale=tau_r[:, t : t + 1])

        den = [tile(f"den{t}", [P, S], F32, "top" if t == 0 else None) for t in range(R)]
        den_sq1 = tile("den_sq1", [P, S], F32)
        den_sq23 = tile("den_sq23", [P, 2, S], F32)
        den_sq = {1: den_sq1[:], 2: den_sq23[:, 0, :], 3: den_sq23[:, 1, :]}
        inv0 = tile("inv0", [P, S], F32)
        for t in range(R):
            for c0, c1 in HALVES:
                nc.vector.scalar_tensor_tensor(den[t][:, c0:c1], ea[t][:, c0:c1], 0.125, ea2[t][:, c0:c1],
                                               ALU.add, ALU.add)
            for c0, c1 in HALVES:
                if t == 0:
                    nc.vector.reciprocal(inv0[:, c0:c1], den[t][:, c0:c1])
                else:
                    nc.vector.tensor_tensor(den_sq[t][:, c0:c1], den[t][:, c0:c1], den[t][:, c0:c1], ALU.mult)

        res = [tile(f"res{c0}", [P, R, HALF], F32) for c0, c1 in HALVES]
        res_bf = [tile(f"res_bf{c0}", [P, HALF, R], BF16) for c0, c1 in HALVES]
        out_w = tile("out_w", [P, S], U32)
        out_s = tile("out_s", [P, S], U8)
        out_rows = out_0.rearrange("(p t) n -> p t n", t=R)
        out_words = out_1[0].rearrange("p n t -> p (n t)").bitcast(I32)
        out_scales = out_2[0].bitcast(I32)

        def normalised(t, inv):
            share = tile(f"share{t}", [P, S], F32)
            share2 = tile(f"share2_{t}", [P, S], F32)
            nc.vector.tensor_tensor(share[:], ea[t][:], inv, ALU.mult)
            nc.vector.tensor_tensor(share2[:], ea2[t][:], inv, ALU.mult)
            return share, share2

        def out_chain(t, c0, c1, weights, s_n3, s_n4, inv=None):
            prod = tile(f"prod{t}_{c0}", [P, c1 - c0], F32)
            prod2 = tile(f"prod2_{t}_{c0}", [P, c1 - c0], F32)

            def fetch_product(dst, weight, lst, fetched):
                nc.scalar.activation(fetched, s_win[t][:].indirect(entries(lst, c0, c1)), ACT.Copy)
                nc.vector.tensor_tensor(dst[:], weight[:, c0:c1], fetched, ALU.mult)

            def combine(in0, in1, op):
                for h, (h0, h1) in enumerate(HALVES):
                    lo, hi = max(c0, h0), min(c1, h1)
                    if lo < hi:
                        nc.vector.tensor_tensor(res[h][:, t, lo - h0 : hi - h0], in0[:, lo - c0 : hi - c0],
                                                in1[:, lo - c0 : hi - c0], op)
                        if hi == h1:
                            nc.sync.dma_start(out_rows[:, t, h0:h1], res[h][:, t, :])

            stages = [
                lambda: fetch_product(prod, weights[0], n3_l, s_n3),
                lambda: fetch_product(prod2, weights[1], n4_l, s_n4),
            ]
            if inv is None:
                return stages + [lambda: combine(prod, prod2, ALU.add)]
            num = tile(f"num{t}", [P, S], F32)
            return stages + [
                lambda: nc.vector.tensor_tensor(num[:], prod[:], prod2[:], ALU.add),
                lambda: combine(num, inv, ALU.mult),
            ]

        s0_fetched = tile("s0_fetched", [P, 2, S], F32, f"exp_bias{LAST}")
        for stage_call in out_chain(0, 0, S, (ea[0], ea2[0]), s0_fetched[:, 0, :], s0_fetched[:, 1, :], inv0):
            stage_call()
        inv23 = tile("inv23", [P, 2, S], F32)
        nc.scalar.activation(inv23[:], den_sq23[:], ACT.Abs_reciprocal_sqrt)
        inv1 = den_sq[3]
        nc.scalar.activation(inv1, den_sq[1], ACT.Abs_reciprocal_sqrt)
        shares = {t: normalised(t, inv23[:, t - 2, :]) for t in (2, 3)}

        tile1 = out_chain(1, 0, S, (ea[1], ea2[1]), den_sq[1], den[3][:], inv1)
        for stage_call in tile1[:3]:
            stage_call()
        chains = [
            [None, None, tile1[3]],
            out_chain(2, 0, HALF, shares[2], den_sq[2][:, :HALF], den_sq[1][:, :HALF]),
            out_chain(3, 0, HALF, shares[3], den_sq[2][:, HALF:], den[3][:, :HALF]),
            out_chain(2, HALF, S, shares[2], den_sq[1][:, HALF:], den[3][:, HALF:]),
        ]
        for c0, c1 in CHUNKS[1:]:
            quarter = slice(c0 - HALF, c1 - HALF)
            chains.append(out_chain(3, c0, c1, shares[3], den_sq[2][:, quarter], den_sq[1][:, quarter]))
            chains[-1].append(
                lambda cols=quarter: interleave(nc.vector.tensor_copy, res_bf[1][:, cols, :], res[1][:, :, cols])
            )
        run_staggered(chains)
        interleave(nc.scalar.copy, res_bf[0][:], res[0][:])
        for h, (c0, c1) in enumerate(HALVES):
            quantise(out_w[:, c0:c1], out_s[:, c0:c1], res_bf[h][:])
            nc.sync.dma_start(out_words[:, c0:c1], out_w[:, c0:c1].bitcast(I32))
        for q in range(4):
            queue = nc.scalar if q % 2 else nc.sync
            queue.dma_start(out_scales[4 * q : 4 * q + 4, :], out_s[32 * q : 32 * q + 4, :].bitcast(I32))
